import numpy as np
import ml_dtypes


def mxq(x, axis, fmt="e4m3"):
    dtype, down = {"e4m3": (ml_dtypes.float8_e4m3fn, 7), "e5m2": (ml_dtypes.float8_e5m2, 14)}[fmt]
    v = np.moveaxis(np.asarray(x, np.float32).astype(ml_dtypes.bfloat16).astype(np.float64), axis, -1)
    blocks = v.reshape(v.shape[:-1] + (-1, 32))
    amax = np.abs(blocks).max(-1, keepdims=True)
    byte = np.maximum(np.where(amax > 0, np.frexp(amax)[1] - 1 + 127, 0) - down, 1)
    scale = np.exp2(byte - 127.0)
    codes = (blocks / scale).astype(np.float32).astype(dtype).astype(np.float64)
    return np.moveaxis((codes * scale).reshape(v.shape), -1, axis)


WIDE = False


def mx_kscale(k):
    if not WIDE:
        return np.ones(k)
    levels = np.array([10, -10, 5, -5, 0])
    if k % 512:
        return np.exp2(np.random.permutation(np.resize(levels, k // 32))).repeat(32)
    a = np.empty((k // 512, 16))
    for p in range(k // 512):
        a[p, :8] = np.random.permutation(np.resize(levels, 8))
        for g in range(8):
            far = levels[np.abs(levels - a[p, g]) >= 10]
            a[p, g + 8] = far[np.random.randint(len(far))]
    return np.exp2(a.ravel()).repeat(32)


def f64(x):
    return np.asarray(x).astype(np.float64)


def striped(idx):
    return np.tile(idx.reshape(-1, 16).T, (8, 1)).astype(np.uint16)


def unstriped(offs):
    return offs[:16].T.reshape(-1).astype(np.int64)


def pack_weight(w):
    k, n = w.shape
    w = f64(np.asarray(w, np.float32).astype(ml_dtypes.bfloat16)).reshape(k // 32, 32, n)
    amax = np.abs(w).max(1)
    byte = np.clip(np.where(amax > 0, np.frexp(amax)[1] - 1 + 127 - 7, 1), 1, 254)
    scaled = (w * np.exp2(127.0 - byte)[:, None, :]).reshape(k, n).astype(np.float32)
    words = np.ascontiguousarray(scaled.reshape(k // 512, 128, 4, n).transpose(0, 1, 3, 2)).astype(ml_dtypes.float8_e4m3fn).view(np.uint8)
    return words, np.ascontiguousarray(byte.astype(np.uint8).reshape(k // 512, 16, n))


def unpack_weight(words, scales):
    g, p, n, _ = words.shape
    vals = np.ascontiguousarray(words).view(ml_dtypes.float8_e4m3fn).astype(np.float64) * np.repeat(np.exp2(scales.astype(np.float64) - 127.0), 8, axis=1)[..., None]
    return vals.transpose(0, 1, 3, 2).reshape(g * 512, n)


def silu(v):
    return v / (1.0 + np.exp(-np.maximum(v, -700.0)))


K, T, S, H, N = 512, 2048, 1024, 512, 256
P = 2 ** 7


def setup_inputs():
    n = np.random.standard_normal
    s = mx_kscale(K)[:, None]
    u = mx_kscale(H)
    packed_w2 = pack_weight(n((H, N)) / np.sqrt(H) / u[:, None])
    return {
        "xT": (n((K, T)) * s).astype(np.float32),
        "gate": np.tile(np.random.uniform(0.2, 1.0, T), (P, 1)).astype(np.float32),
        "w1": (n((K, H)) / np.sqrt(K) / s * u).astype(np.float32),
        "w2_words": packed_w2[0],
        "w2_scales": packed_w2[1],
        "offs": striped(np.random.permutation(T)[:S]),
    }


def reference(xT, gate, w1, w2_words, w2_scales, offs):
    xq = mxq(f64(xT)[:, unstriped(offs)], 0, "e4m3")
    h = silu(mxq(f64(w1), 0, "e4m3").T @ xq)
    y = unpack_weight(w2_words, w2_scales).T @ mxq(h, 0, "e4m3")
    g = f64(gate)[:1][:, unstriped(offs)]
    out = np.zeros((N, T))
    out[:, unstriped(offs)] = y * g
    return out

@@ -1,0 +1,194 @@
+from contextlib import ExitStack
+
+import concourse.mybir as mybir
+from concourse.masks import make_identity
+
+K, T, S, H, N = 512, 2048, 1024, 512, 256
+FLOPS = 2 * S * (K * H + H * N)
+
+F32 = mybir.dt.float32
+BF16 = mybir.dt.bfloat16
+I32 = mybir.dt.int32
+U32 = mybir.dt.uint32
+U16 = mybir.dt.uint16
+U8 = mybir.dt.uint8
+FP8X4 = mybir.dt.float8_e4m3fn_x4
+MULT = mybir.AluOpType.mult
+SILU = mybir.ActivationFunctionType.Silu
+
+P = 128
+PACK = 4
+CHUNK = 256
+CHUNKS = S // CHUNK
+HALF = 128
+LIST_COLS = CHUNK // 16
+LOADS = (((0, 512), (512, 1024), (1024, 1536), (1536, 2048)),
+         ((0, 512), (512, 1024), (1024, 1536), (1536, 1792), (1792, 2048)))
+ON_VECTOR = (2048, 1536)
+W1_ON_SCALAR = 48
+SHARED = 512
+
+
+def tile_picked_modgate_mlpsilu_l_kernel(tc, xT, gate, w1, w2_words, w2_scales, offs, out):
+    nc = tc.nc
+    with ExitStack() as ctx:
+        keep = ctx.enter_context(tc.tile_pool(name="keep", bufs=1))
+        psum = ctx.enter_context(tc.psum_pool(name="psum", bufs=1))
+
+        gate_cols = keep.tile([P, 16], F32, name="gate_cols")
+        nc.sync.dma_start(out=gate_cols[:], in_=gate[0].rearrange("(p m) -> p m", m=16))
+        w1_raw = keep.tile([P, PACK, H], F32, name="w1_raw")
+        nc.sync.dma_start(out=w1_raw[:], in_=w1.rearrange("(p j) c -> p j c", j=PACK))
+        offsets = keep.tile([P, S // 16], U16, name="offsets")
+        nc.sync.dma_start(offsets[:], offs)
+        x_rows = xT.rearrange("(p t) c -> p t c", t=PACK)
+        x_raw = {}
+        for u in range(2):
+            for a, b in LOADS[u]:
+                raw = keep.tile([P, 2, b - a], F32, name=f"x_raw{u}_{a}")
+                nc.sync.dma_start(out=raw[:], in_=x_rows[:, 2 * u : 2 * u + 2, a:b])
+                x_raw[u, a] = raw
+        w2_codes = keep.tile([P, N], U32, name="w2_codes", align_bytes=64)
+        nc.sync.dma_start(out=w2_codes[:].bitcast(I32), in_=w2_words[0].rearrange("p n t -> p (n t)").bitcast(I32))
+        w2_plane = keep.tile([P, N], U8, name="w2_plane", align_bytes=64)
+        nc.vector.memset(w2_plane[:].bitcast(U32), 0)
+        for q in range(4):
+            nc.sync.dma_start(out=w2_plane[32 * q : 32 * q + 4, :].bitcast(I32), in_=w2_scales[0, 4 * q : 4 * q + 4, :].bitcast(I32))
+
+        warm = keep.tile([P, 8], F32, name="warm")
+        warm_out = keep.tile([P, 8], F32, name="warm_out")
+        nc.vector.memset(warm[:], 0.0)
+        nc.scalar.activation(out=warm_out[:], in_=warm[:], func=SILU)
+        identity = keep.tile([P, P], F32, name="identity")
+        make_identity(nc, identity[:])
+
+        placed = [keep.tile([P, T], F32, name=f"placed{r}") for r in range(2)]
+        for r in range(2):
+            nc.vector.memset(placed[r][:].bitcast(I32), 0)
+
+        gate_table = keep.tile([P, T], F32, name="gate_table", tag="table")
+        for a in range(4):
+            bank = psum.tile([P, 4, P], F32, name=f"gate_bank{a}", tag="hidden", bufs=4)
+            for b in range(4):
+                m = 4 * a + b
+                nc.tensor.transpose(bank[:, b, :], gate_cols[:, m : m + 1].to_broadcast([P, P]), identity[:])
+            dst = gate_table[:].rearrange("p (n a b) -> p a n b", a=4, b=4)[:, a]
+            if a == 0:
+                nc.scalar.copy(out=dst, in_=bank[:].rearrange("p b n -> p n b"))
+            else:
+                nc.vector.tensor_copy(out=dst, in_=bank[:].rearrange("p b n -> p n b"))
+
+        w1_bf = keep.tile([P, PACK * H], BF16, name="w1_bf", align_bytes=64)
+        w1_dst = w1_bf[:].rearrange("p (t m j) -> p m j t", t=PACK, j=PACK)
+        w1_src = w1_raw[:].rearrange("p j (m t) -> p m j t", t=PACK)
+        nc.scalar.copy(out=w1_dst[:, :W1_ON_SCALAR], in_=w1_src[:, :W1_ON_SCALAR])
+        nc.vector.tensor_copy(out=w1_dst[:, W1_ON_SCALAR:], in_=w1_src[:, W1_ON_SCALAR:])
+        w1_codes = keep.tile([P, H], U32, name="w1_codes", align_bytes=64)
+        w1_plane = keep.tile([P, H], U8, name="w1_plane", align_bytes=64)
+        nc.vector.quantize_mx(out=w1_codes[:].bitcast(FP8X4), scales=w1_plane[:], in_=w1_bf[:])
+
+        gate_picked = keep.tile([P, S], F32, name="gate_picked")
+        nc.vector.tensor_copy(out=gate_picked[:], in_=gate_table[:].indirect(offsets[:]))
+
+        tables = keep.tile([P, 2 * (2 * T - SHARED)], BF16, name="tables")
+        pairs = [tables[:, 2 * (T - SHARED) :], tables[:, : 2 * T]]
+        staged = keep.tile([P, 6 * CHUNK], U32, name="staged", tag="table")
+        slots = staged[:].rearrange("p (r s) -> p r s", s=CHUNK)
+        LOW = (2, 3, 0, 1)
+        HIGH = (4, 5, 3, 5)
+
+        def round_pairs(u):
+            for a, b in LOADS[u]:
+                dst = pairs[u][:, 2 * a : 2 * b].rearrange("p (c e) -> p c e", e=2)
+                src = x_raw[u, a][:].rearrange("p e c -> p c e")
+                if a >= ON_VECTOR[u]:
+                    nc.vector.tensor_copy(out=dst, in_=src)
+                else:
+                    nc.scalar.copy(out=dst, in_=src)
+
+        def entries(c, n=1):
+            return offsets[:, c * LIST_COLS : (c + n) * LIST_COLS]
+
+        round_pairs(0)
+        for c in (0, 2):
+            nc.vector.tensor_copy(out=staged[:, LOW[c] * CHUNK : (LOW[c] + 2) * CHUNK], in_=pairs[0].bitcast(U32).indirect(entries(c, 2)))
+        round_pairs(1)
+
+        y = [keep.tile([P, S], F32, name=f"y{r}") for r in range(2)]
+        x_codes, x_plane, h_bf, y_bank = {}, {}, {}, {}
+
+        def pick(c):
+            nc.vector.tensor_copy(out=slots[:, HIGH[c], :], in_=pairs[1].bitcast(U32).indirect(entries(c)))
+
+        def weave(c):
+            picked = keep.tile([P, PACK * CHUNK], BF16, name=f"picked{c}", align_bytes=64)
+            both = slots[:, LOW[c] : HIGH[c] + 1 : HIGH[c] - LOW[c], :]
+            nc.scalar.copy(out=picked[:].bitcast(U32).rearrange("p (s u) -> p s u", u=2), in_=both.rearrange("p u s -> p s u"))
+            x_codes[c] = keep.tile([P, CHUNK], U32, name=f"x_codes{c}", align_bytes=64)
+            x_plane[c] = keep.tile([P, CHUNK], U8, name=f"x_plane{c}", align_bytes=64)
+            nc.vector.quantize_mx(out=x_codes[c][:].bitcast(FP8X4), scales=x_plane[c][:], in_=picked[:])
+            h_bf[c] = keep.tile([P, PACK * CHUNK], BF16, name=f"h_bf{c}", align_bytes=64)
+
+        def hidden(c, g):
+            cols = slice(g * HALF, (g + 1) * HALF)
+            bank = psum.tile([P, PACK, HALF], F32, name=f"h_bank{c}_{g}", tag="hidden", bufs=4)
+            for t in range(PACK):
+                chans = slice(t * P, (t + 1) * P)
+                nc.tensor.matmul_mx(out=bank[:, t, :], lhsT=w1_codes[:, chans].bitcast(FP8X4), lhsT_scale=w1_plane[:, chans],
+                                    rhs=x_codes[c][:, cols].bitcast(FP8X4), rhs_scale=x_plane[c][:, cols], start=True, stop=True)
+            dst = h_bf[c][:, g * PACK * HALF : (g + 1) * PACK * HALF].rearrange("p (n t) -> p n t", t=PACK)
+            nc.scalar.activation(out=dst, in_=bank[:].rearrange("p t n -> p n t"), func=SILU)
+
+        def second_layer(c):
+            h_codes = keep.tile([P, CHUNK], U32, name=f"h_codes{c}", align_bytes=64)
+            h_plane = keep.tile([P, CHUNK], U8, name=f"h_plane{c}", align_bytes=64)
+            nc.vector.quantize_mx(out=h_codes[:].bitcast(FP8X4), scales=h_plane[:], in_=h_bf[c][:])
+            y_bank[c] = psum.tile([P, 2, CHUNK], F32, name=f"y_bank{c}", tag="result", bufs=4)
+            for r in range(2):
+                rows = slice(r * P, (r + 1) * P)
+                nc.tensor.matmul_mx(out=y_bank[c][:, r, :], lhsT=w2_codes[:, rows].bitcast(FP8X4), lhsT_scale=w2_plane[:, rows],
+                                    rhs=h_codes[:].bitcast(FP8X4), rhs_scale=h_plane[:], start=True, stop=True)
+
+        def empty(r, c):
+            nc.scalar.copy(out=y[r][:, c * CHUNK : (c + 1) * CHUNK], in_=y_bank[c][:, r, :])
+
+        def place(r, c, n=1):
+            cols = slice(c * CHUNK, (c + n) * CHUNK)
+            nc.vector.tensor_tensor(placed[r][:].indirect(entries(c, n)), y[r][:, cols], gate_picked[:, cols], MULT)
+
+        pick(0)
+        pick(1)
+        weave(0)
+        weave(1)
+        pick(2)
+        pick(3)
+        hidden(0, 0)
+        hidden(0, 1)
+        second_layer(0)
+        weave(2)
+        hidden(1, 0)
+        empty(0, 0)
+        place(0, 0)
+        hidden(1, 1)
+        second_layer(1)
+        weave(3)
+        empty(1, 0)
+        place(1, 0)
+        hidden(2, 0)
+        hidden(2, 1)
+        second_layer(2)
+        empty(0, 1)
+        place(0, 1)
+        hidden(3, 0)
+        hidden(3, 1)
+        second_layer(3)
+        empty(1, 1)
+        place(1, 1)
+        empty(0, 2)
+        empty(0, 3)
+        place(0, 2, 2)
+        nc.sync.dma_start(out=out[0:P, :], in_=placed[0][:])
+        empty(1, 2)
+        empty(1, 3)
+        place(1, 2, 2)
+        nc.sync.dma_start(out=out[P : 2 * P, :], in_=placed[1][:])

@@ -1,7 +1,6 @@
 from contextlib import ExitStack
 
 import concourse.mybir as mybir
-from concourse.masks import make_identity
 
 K, T, S, H, N = 512, 2048, 1024, 512, 256
 FLOPS = 2 * S * (K * H + H * N)
@@ -25,7 +24,6 @@ LIST_COLS = CHUNK // 16
 LOADS = (((0, 512), (512, 1024), (1024, 1536), (1536, 2048)),
          ((0, 512), (512, 1024), (1024, 1536), (1536, 1792), (1792, 2048)))
 ON_VECTOR = (2048, 1536)
-W1_ON_SCALAR = 48
 SHARED = 512
 
 
@@ -59,30 +57,29 @@ def tile_picked_modgate_mlpsilu_l_kernel(tc, xT, gate, w1, w2_words, w2_scales, 
         warm_out = keep.tile([P, 8], F32, name="warm_out")
         nc.vector.memset(warm[:], 0.0)
         nc.scalar.activation(out=warm_out[:], in_=warm[:], func=SILU)
-        identity = keep.tile([P, P], F32, name="identity")
-        make_identity(nc, identity[:])
+        identity = keep.tile([P, P], F32, name="identity", align_bytes=64)
+        zeros = keep.tile([P, P], F32, name="zeros", tag="placed1")
+        nc.gpsimd.memset(zeros[:], 0.0)
+        nc.gpsimd.affine_select(out=identity[:], in_=zeros[:], compare_op=mybir.AluOpType.not_equal, fill=1.0, base=0,
+                                pattern=[[-1, P]], channel_multiplier=1)
 
         placed = [keep.tile([P, T], F32, name=f"placed{r}") for r in range(2)]
-        for r in range(2):
-            nc.vector.memset(placed[r][:].bitcast(I32), 0)
+        nc.vector.memset(placed[0][:].bitcast(I32), 0)
+        nc.gpsimd.memset(placed[1][:].bitcast(I32), 0)
 
-        gate_table = keep.tile([P, T], F32, name="gate_table", tag="table")
+        gate_table = keep.tile([P, T], F32, name="gate_table", tag="table", align_bytes=64)
         for a in range(4):
-            bank = psum.tile([P, 4, P], F32, name=f"gate_bank{a}", tag="hidden", bufs=4)
+            bank = psum.tile([P, 4, P], F32, name=f"gate_bank{a}", tag=f"bank{a}")
             for b in range(4):
                 m = 4 * a + b
                 nc.tensor.transpose(bank[:, b, :], gate_cols[:, m : m + 1].to_broadcast([P, P]), identity[:])
             dst = gate_table[:].rearrange("p (n a b) -> p a n b", a=4, b=4)[:, a]
-            if a == 0:
-                nc.scalar.copy(out=dst, in_=bank[:].rearrange("p b n -> p n b"))
-            else:
-                nc.vector.tensor_copy(out=dst, in_=bank[:].rearrange("p b n -> p n b"))
+            nc.vector.tensor_copy(out=dst, in_=bank[:].rearrange("p b n -> p n b"))
 
-        w1_bf = keep.tile([P, PACK * H], BF16, name="w1_bf", align_bytes=64)
-        w1_dst = w1_bf[:].rearrange("p (t m j) -> p m j t", t=PACK, j=PACK)
-        w1_src = w1_raw[:].rearrange("p j (m t) -> p m j t", t=PACK)
-        nc.scalar.copy(out=w1_dst[:, :W1_ON_SCALAR], in_=w1_src[:, :W1_ON_SCALAR])
-        nc.vector.tensor_copy(out=w1_dst[:, W1_ON_SCALAR:], in_=w1_src[:, W1_ON_SCALAR:])
+        w1_bf = keep.tile([P, PACK * H], BF16, name="w1_bf", tag="identity", align_bytes=64)
+        w1_dst = w1_bf[:].rearrange("p (t m j) -> p m t j", t=PACK, j=PACK)
+        w1_src = w1_raw[:].rearrange("p j (m t) -> p m t j", t=PACK)
+        nc.vector.tensor_copy(out=w1_dst, in_=w1_src)
         w1_codes = keep.tile([P, H], U32, name="w1_codes", align_bytes=64)
         w1_plane = keep.tile([P, H], U8, name="w1_plane", align_bytes=64)
         nc.vector.quantize_mx(out=w1_codes[:].bitcast(FP8X4), scales=w1_plane[:], in_=w1_bf[:])
@@ -92,10 +89,9 @@ def tile_picked_modgate_mlpsilu_l_kernel(tc, xT, gate, w1, w2_words, w2_scales, 
 
         tables = keep.tile([P, 2 * (2 * T - SHARED)], BF16, name="tables")
         pairs = [tables[:, 2 * (T - SHARED) :], tables[:, : 2 * T]]
-        staged = keep.tile([P, 6 * CHUNK], U32, name="staged", tag="table")
-        slots = staged[:].rearrange("p (r s) -> p r s", s=CHUNK)
-        LOW = (2, 3, 0, 1)
-        HIGH = (4, 5, 3, 5)
+        staged = keep.tile([P, 6 * CHUNK], U32, name="staged", tag="table", align_bytes=64)
+        REST = S - CHUNK
+        first_words = staged[:, REST + CHUNK :]
 
         def round_pairs(u):
             for a, b in LOADS[u]:
@@ -109,29 +105,31 @@ def tile_picked_modgate_mlpsilu_l_kernel(tc, xT, gate, w1, w2_words, w2_scales, 
         def entries(c, n=1):
             return offsets[:, c * LIST_COLS : (c + n) * LIST_COLS]
 
+        def pick_first(u):
+            nc.vector.tensor_copy(out=first_words.rearrange("p (s u) -> p s u", u=2)[:, :, u], in_=pairs[u].bitcast(U32).indirect(entries(0)))
+
+        def pick(u, c, n):
+            start = u * REST + (c - 1) * CHUNK
+            nc.vector.tensor_copy(out=staged[:, start : start + n * CHUNK], in_=pairs[u].bitcast(U32).indirect(entries(c, n)))
+
         round_pairs(0)
-        for c in (0, 2):
-            nc.vector.tensor_copy(out=staged[:, LOW[c] * CHUNK : (LOW[c] + 2) * CHUNK], in_=pairs[0].bitcast(U32).indirect(entries(c, 2)))
+        pick_first(0)
+        pick(0, 1, 3)
         round_pairs(1)
 
         y = [keep.tile([P, S], F32, name=f"y{r}") for r in range(2)]
-        x_codes, x_plane, h_bf, y_bank = {}, {}, {}, {}
+        x_codes = [keep.tile([P, CHUNK], U32, name=f"x_codes{c}", align_bytes=64) for c in range(CHUNKS)]
+        x_plane = [keep.tile([P, CHUNK], U8, name=f"x_plane{c}", align_bytes=64) for c in range(CHUNKS)]
+        h_bf = [keep.tile([P, PACK * CHUNK], BF16, name=f"h_bf{c}", align_bytes=64) for c in range(CHUNKS)]
+        h_codes = [keep.tile([P, CHUNK], U32, name=f"h_codes{c}", align_bytes=64) for c in range(CHUNKS)]
+        h_plane = [keep.tile([P, CHUNK], U8, name=f"h_plane{c}", align_bytes=64) for c in range(CHUNKS)]
 
-        def pick(c):
-            nc.vector.tensor_copy(out=slots[:, HIGH[c], :], in_=pairs[1].bitcast(U32).indirect(entries(c)))
+        def quantize(codes, plane, values, a, b):
+            nc.vector.quantize_mx(out=codes[:, a:b].bitcast(FP8X4), scales=plane[:, a:b], in_=values[:, PACK * a : PACK * b])
 
-        def weave(c):
-            picked = keep.tile([P, PACK * CHUNK], BF16, name=f"picked{c}", align_bytes=64)
-            both = slots[:, LOW[c] : HIGH[c] + 1 : HIGH[c] - LOW[c], :]
-            nc.scalar.copy(out=picked[:].bitcast(U32).rearrange("p (s u) -> p s u", u=2), in_=both.rearrange("p u s -> p s u"))
-            x_codes[c] = keep.tile([P, CHUNK], U32, name=f"x_codes{c}", align_bytes=64)
-            x_plane[c] = keep.tile([P, CHUNK], U8, name=f"x_plane{c}", align_bytes=64)
-            nc.vector.quantize_mx(out=x_codes[c][:].bitcast(FP8X4), scales=x_plane[c][:], in_=picked[:])
-            h_bf[c] = keep.tile([P, PACK * CHUNK], BF16, name=f"h_bf{c}", align_bytes=64)
-
-        def hidden(c, g):
+        def hidden(c, g, tag):
             cols = slice(g * HALF, (g + 1) * HALF)
-            bank = psum.tile([P, PACK, HALF], F32, name=f"h_bank{c}_{g}", tag="hidden", bufs=4)
+            bank = psum.tile([P, PACK, HALF], F32, name=f"h_bank{c}_{g}", tag=tag)
             for t in range(PACK):
                 chans = slice(t * P, (t + 1) * P)
                 nc.tensor.matmul_mx(out=bank[:, t, :], lhsT=w1_codes[:, chans].bitcast(FP8X4), lhsT_scale=w1_plane[:, chans],
@@ -139,56 +137,65 @@ def tile_picked_modgate_mlpsilu_l_kernel(tc, xT, gate, w1, w2_words, w2_scales, 
             dst = h_bf[c][:, g * PACK * HALF : (g + 1) * PACK * HALF].rearrange("p (n t) -> p n t", t=PACK)
             nc.scalar.activation(out=dst, in_=bank[:].rearrange("p t n -> p n t"), func=SILU)
 
-        def second_layer(c):
-            h_codes = keep.tile([P, CHUNK], U32, name=f"h_codes{c}", align_bytes=64)
-            h_plane = keep.tile([P, CHUNK], U8, name=f"h_plane{c}", align_bytes=64)
-            nc.vector.quantize_mx(out=h_codes[:].bitcast(FP8X4), scales=h_plane[:], in_=h_bf[c][:])
-            y_bank[c] = psum.tile([P, 2, CHUNK], F32, name=f"y_bank{c}", tag="result", bufs=4)
-            for r in range(2):
-                rows = slice(r * P, (r + 1) * P)
-                nc.tensor.matmul_mx(out=y_bank[c][:, r, :], lhsT=w2_codes[:, rows].bitcast(FP8X4), lhsT_scale=w2_plane[:, rows],
-                                    rhs=h_codes[:].bitcast(FP8X4), rhs_scale=h_plane[:], start=True, stop=True)
-
-        def empty(r, c):
-            nc.scalar.copy(out=y[r][:, c * CHUNK : (c + 1) * CHUNK], in_=y_bank[c][:, r, :])
+        def result(dst, r, c, a, b):
+            rows = slice(r * P, (r + 1) * P)
+            nc.tensor.matmul_mx(out=dst, lhsT=w2_codes[:, rows].bitcast(FP8X4), lhsT_scale=w2_plane[:, rows],
+                                rhs=h_codes[c][:, a:b].bitcast(FP8X4), rhs_scale=h_plane[c][:, a:b], start=True, stop=True)
 
         def place(r, c, n=1):
             cols = slice(c * CHUNK, (c + n) * CHUNK)
             nc.vector.tensor_tensor(placed[r][:].indirect(entries(c, n)), y[r][:, cols], gate_picked[:, cols], MULT)
 
-        pick(0)
-        pick(1)
-        weave(0)
-        weave(1)
-        pick(2)
-        pick(3)
-        hidden(0, 0)
-        hidden(0, 1)
-        second_layer(0)
-        weave(2)
-        hidden(1, 0)
-        empty(0, 0)
+        halves = staged[:].rearrange("p (u s) -> p s u", u=2)
+
+        def weave(c, picked):
+            a, b = (c - 1) * CHUNK, c * CHUNK
+            nc.scalar.copy(out=picked.bitcast(U32).rearrange("p (s u) -> p s u", u=2), in_=halves[:, a:b, :])
+            quantize(x_codes[c], x_plane[c], picked, 0, CHUNK)
+
+        def empty(bank, r, c, n=1):
+            nc.scalar.copy(out=y[r][:, c * CHUNK : (c + n) * CHUNK], in_=bank)
+
+        def held(r, c, tag):
+            bank = psum.tile([P, CHUNK], F32, name=f"y_bank{r}_{c}", tag=tag)
+            result(bank[:], r, c, 0, CHUNK)
+            empty(bank[:], r, c)
+            place(r, c)
+
+        pick_first(1)
+        pick(1, 1, 1)
+        y_first = psum.tile([P, CHUNK], F32, name="y_first", tag="bank4")
+        for g in range(2):
+            quantize(x_codes[0], x_plane[0], first_words.bitcast(BF16), g * HALF, (g + 1) * HALF)
+        picked_second = keep.tile([P, PACK * CHUNK], BF16, name="picked_second", align_bytes=64)
+        weave(1, picked_second[:])
+        pick(1, 2, 2)
+        for g in range(2):
+            hidden(0, g, f"bank{g}")
+            quantize(h_codes[0], h_plane[0], h_bf[0], g * HALF, (g + 1) * HALF)
+            result(y_first[:, g * HALF : (g + 1) * HALF], 0, 0, g * HALF, (g + 1) * HALF)
+        nc.vector.tensor_copy(out=y[0][:, :CHUNK], in_=y_first[:])
+
+        picked_rest = keep.tile([P, 2 * PACK * CHUNK], BF16, name="picked_rest", tag="x_codes0", align_bytes=64)
+        weave(2, picked_rest[:, : PACK * CHUNK])
+        weave(3, picked_rest[:, PACK * CHUNK :])
         place(0, 0)
-        hidden(1, 1)
-        second_layer(1)
-        weave(3)
-        empty(1, 0)
-        place(1, 0)
-        hidden(2, 0)
-        hidden(2, 1)
-        second_layer(2)
-        empty(0, 1)
-        place(0, 1)
-        hidden(3, 0)
-        hidden(3, 1)
-        second_layer(3)
-        empty(1, 1)
-        place(1, 1)
-        empty(0, 2)
-        empty(0, 3)
-        place(0, 2, 2)
-        nc.sync.dma_start(out=out[0:P, :], in_=placed[0][:])
-        empty(1, 2)
-        empty(1, 3)
-        place(1, 2, 2)
-        nc.sync.dma_start(out=out[P : 2 * P, :], in_=placed[1][:])
+        hidden(1, 0, "bank2")
+        hidden(1, 1, "bank3")
+        quantize(h_codes[1], h_plane[1], h_bf[1], 0, CHUNK)
+        hidden(2, 0, "bank0")
+        held(1, 0, "bank3")
+        hidden(2, 1, "bank1")
+        quantize(h_codes[2], h_plane[2], h_bf[2], 0, CHUNK)
+        hidden(3, 0, "bank5")
+        held(0, 1, "bank1")
+        hidden(3, 1, "bank4")
+        quantize(h_codes[3], h_plane[3], h_bf[3], 0, CHUNK)
+        held(1, 1, "bank4")
+        for r in range(2):
+            y_last = psum.tile([P, 2, CHUNK], F32, name=f"y_last{r}", tag=f"bank{6 + r}")
+            for c in (2, 3):
+                result(y_last[:, c - 2, :], r, c, 0, CHUNK)
+            empty(y_last[:].rearrange("p c s -> p (c s)"), r, 2, 2)
+            place(r, 2, 2)
+            nc.sync.dma_start(out=out[r * P : (r + 1) * P, :], in_=placed[r][:])

@@ -174,11 +174,11 @@ def tile_picked_modgate_mlpsilu_l_kernel(tc, xT, gate, w1, w2_words, w2_scales, 
             hidden(0, g, f"bank{g}")
             quantize(h_codes[0], h_plane[0], h_bf[0], g * HALF, (g + 1) * HALF)
             result(y_first[:, g * HALF : (g + 1) * HALF], 0, 0, g * HALF, (g + 1) * HALF)
-        nc.vector.tensor_copy(out=y[0][:, :CHUNK], in_=y_first[:])
 
         picked_rest = keep.tile([P, 2 * PACK * CHUNK], BF16, name="picked_rest", tag="x_codes0", align_bytes=64)
         weave(2, picked_rest[:, : PACK * CHUNK])
         weave(3, picked_rest[:, PACK * CHUNK :])
+        empty(y_first[:], 0, 0)
         place(0, 0)
         hidden(1, 0, "bank2")
         hidden(1, 1, "bank3")

@@ -76,11 +76,12 @@ def tile_picked_modgate_mlpsilu_l_kernel(tc, xT, gate, w1, w2_words, w2_scales, 
             dst = gate_table[:].rearrange("p (n a b) -> p a n b", a=4, b=4)[:, a]
             nc.vector.tensor_copy(out=dst, in_=bank[:].rearrange("p b n -> p n b"))
 
-        w1_bf = keep.tile([P, PACK * H], BF16, name="w1_bf", tag="identity", align_bytes=64)
-        w1_dst = w1_bf[:].rearrange("p (t m j) -> p m t j", t=PACK, j=PACK)
-        w1_src = w1_raw[:].rearrange("p j (m t) -> p m t j", t=PACK)
-        nc.vector.tensor_copy(out=w1_dst, in_=w1_src)
-        w1_codes = keep.tile([P, H], U32, name="w1_codes", align_bytes=64)
+        w1_bf = keep.tile([P, PACK * H], BF16, name="w1_bf", align_bytes=64)
+        w1_dst = w1_bf[:].rearrange("p (t m j) -> p m j t", t=PACK, j=PACK)
+        w1_src = w1_raw[:].rearrange("p j (m t) -> p m j t", t=PACK)
+        nc.vector.tensor_copy(out=w1_dst[:, :, :, :2], in_=w1_src[:, :, :, :2])
+        nc.scalar.copy(out=w1_dst[:, :, :, 2:], in_=w1_src[:, :, :, 2:])
+        w1_codes = keep.tile([P, H], U32, name="w1_codes", tag="identity", align_bytes=64)
         w1_plane = keep.tile([P, H], U8, name="w1_plane", align_bytes=64)
         nc.vector.quantize_mx(out=w1_codes[:].bitcast(FP8X4), scales=w1_plane[:], in_=w1_bf[:])
 
@@ -95,8 +96,8 @@ def tile_picked_modgate_mlpsilu_l_kernel(tc, xT, gate, w1, w2_words, w2_scales, 
 
         def round_pairs(u):
             for a, b in LOADS[u]:
-                dst = pairs[u][:, 2 * a : 2 * b].rearrange("p (c e) -> p c e", e=2)
-                src = x_raw[u, a][:].rearrange("p e c -> p c e")
+                dst = pairs[u][:, 2 * a : 2 * b].rearrange("p (c i e) -> p c e i", i=4, e=2)
+                src = x_raw[u, a][:].rearrange("p e (c i) -> p c e i", i=4)
                 if a >= ON_VECTOR[u]:
                     nc.vector.tensor_copy(out=dst, in_=src)
                 else:
@@ -146,11 +147,11 @@ def tile_picked_modgate_mlpsilu_l_kernel(tc, xT, gate, w1, w2_words, w2_scales, 
             cols = slice(c * CHUNK, (c + n) * CHUNK)
             nc.vector.tensor_tensor(placed[r][:].indirect(entries(c, n)), y[r][:, cols], gate_picked[:, cols], MULT)
 
-        halves = staged[:].rearrange("p (u s) -> p s u", u=2)
+        halves = staged[:].rearrange("p (u s i) -> p s u i", u=2, i=4)
 
         def weave(c, picked):
             a, b = (c - 1) * CHUNK, c * CHUNK
-            nc.scalar.copy(out=picked.bitcast(U32).rearrange("p (s u) -> p s u", u=2), in_=halves[:, a:b, :])
+            nc.scalar.copy(out=picked.bitcast(U32).rearrange("p (s i u) -> p s u i", i=4, u=2), in_=halves[:, a // 4 : b // 4])
             quantize(x_codes[c], x_plane[c], picked, 0, CHUNK)
 
         def empty(bank, r, c, n=1):

@@ -21,10 +21,8 @@ CHUNK = 256
 CHUNKS = S // CHUNK
 HALF = 128
 LIST_COLS = CHUNK // 16
-LOADS = (((0, 512), (512, 1024), (1024, 1536), (1536, 2048)),
-         ((0, 512), (512, 1024), (1024, 1536), (1536, 1792), (1792, 2048)))
-ON_VECTOR = (2048, 1536)
-SHARED = 512
+LOADS = (((0, 1024, 0), (1024, 2048, 2048)),
+         ((0, 1024, 896), (1024, 1664, 1024), (1664, 2048, 1664)))
 
 
 def tile_picked_modgate_mlpsilu_l_kernel(tc, xT, gate, w1, w2_words, w2_scales, offs, out):
@@ -33,19 +31,26 @@ def tile_picked_modgate_mlpsilu_l_kernel(tc, xT, gate, w1, w2_words, w2_scales, 
         keep = ctx.enter_context(tc.tile_pool(name="keep", bufs=1))
         psum = ctx.enter_context(tc.psum_pool(name="psum", bufs=1))
 
-        gate_cols = keep.tile([P, 16], F32, name="gate_cols")
-        nc.sync.dma_start(out=gate_cols[:], in_=gate[0].rearrange("(p m) -> p m", m=16))
-        w1_raw = keep.tile([P, PACK, H], F32, name="w1_raw")
-        nc.sync.dma_start(out=w1_raw[:], in_=w1.rearrange("(p j) c -> p j c", j=PACK))
+        tables = [keep.tile([P, T], F32, name=f"table{u}", align_bytes=64) for u in range(2)]
+        pairs = [table[:].bitcast(BF16) for table in tables]
+        gate_table = tables[1][:]
+        gate_cols = tables[0][:, T - 16 :]
+        nc.sync.dma_start(out=gate_cols, in_=gate[0].rearrange("(p m) -> p m", m=16))
         offsets = keep.tile([P, S // 16], U16, name="offsets")
         nc.sync.dma_start(offsets[:], offs)
         x_rows = xT.rearrange("(p t) c -> p t c", t=PACK)
         x_raw = {}
-        for u in range(2):
-            for a, b in LOADS[u]:
+
+        def load_pair(u):
+            for a, b, cut in LOADS[u]:
                 raw = keep.tile([P, 2, b - a], F32, name=f"x_raw{u}_{a}")
                 nc.sync.dma_start(out=raw[:], in_=x_rows[:, 2 * u : 2 * u + 2, a:b])
                 x_raw[u, a] = raw
+
+        load_pair(0)
+        w1_raw = keep.tile([P, PACK, H], F32, name="w1_raw")
+        nc.sync.dma_start(out=w1_raw[:], in_=w1.rearrange("(p j) c -> p j c", j=PACK))
+        load_pair(1)
         w2_codes = keep.tile([P, N], U32, name="w2_codes", align_bytes=64)
         nc.sync.dma_start(out=w2_codes[:].bitcast(I32), in_=w2_words[0].rearrange("p n t -> p (n t)").bitcast(I32))
         w2_plane = keep.tile([P, N], U8, name="w2_plane", align_bytes=64)
@@ -67,41 +72,27 @@ def tile_picked_modgate_mlpsilu_l_kernel(tc, xT, gate, w1, w2_words, w2_scales, 
         nc.vector.memset(placed[0][:].bitcast(I32), 0)
         nc.gpsimd.memset(placed[1][:].bitcast(I32), 0)
 
-        gate_table = keep.tile([P, T], F32, name="gate_table", tag="table", align_bytes=64)
         for a in range(4):
             bank = psum.tile([P, 4, P], F32, name=f"gate_bank{a}", tag=f"bank{a}")
             for b in range(4):
                 m = 4 * a + b
                 nc.tensor.transpose(bank[:, b, :], gate_cols[:, m : m + 1].to_broadcast([P, P]), identity[:])
-            dst = gate_table[:].rearrange("p (n a b) -> p a n b", a=4, b=4)[:, a]
-            nc.vector.tensor_copy(out=dst, in_=bank[:].rearrange("p b n -> p n b"))
-
-        w1_bf = keep.tile([P, PACK * H], BF16, name="w1_bf", align_bytes=64)
-        w1_dst = w1_bf[:].rearrange("p (t m j) -> p m j t", t=PACK, j=PACK)
-        w1_src = w1_raw[:].rearrange("p j (m t) -> p m j t", t=PACK)
-        nc.vector.tensor_copy(out=w1_dst[:, :, :, :2], in_=w1_src[:, :, :, :2])
-        nc.scalar.copy(out=w1_dst[:, :, :, 2:], in_=w1_src[:, :, :, 2:])
-        w1_codes = keep.tile([P, H], U32, name="w1_codes", tag="identity", align_bytes=64)
-        w1_plane = keep.tile([P, H], U8, name="w1_plane", align_bytes=64)
-        nc.vector.quantize_mx(out=w1_codes[:].bitcast(FP8X4), scales=w1_plane[:], in_=w1_bf[:])
+            dst = gate_table.rearrange("p (n a b) -> p a n b", a=4, b=4)[:, a]
+            nc.scalar.copy(out=dst, in_=bank[:].rearrange("p b n -> p n b"))
 
         gate_picked = keep.tile([P, S], F32, name="gate_picked")
-        nc.vector.tensor_copy(out=gate_picked[:], in_=gate_table[:].indirect(offsets[:]))
+        nc.vector.tensor_copy(out=gate_picked[:], in_=gate_table.indirect(offsets[:]))
 
-        tables = keep.tile([P, 2 * (2 * T - SHARED)], BF16, name="tables")
-        pairs = [tables[:, 2 * (T - SHARED) :], tables[:, : 2 * T]]
-        staged = keep.tile([P, 6 * CHUNK], U32, name="staged", tag="table", align_bytes=64)
+        staged = keep.tile([P, 6 * CHUNK], U32, name="staged", align_bytes=64)
         REST = S - CHUNK
         first_words = staged[:, REST + CHUNK :]
 
         def round_pairs(u):
-            for a, b in LOADS[u]:
-                dst = pairs[u][:, 2 * a : 2 * b].rearrange("p (c i e) -> p c e i", i=4, e=2)
-                src = x_raw[u, a][:].rearrange("p e (c i) -> p c e i", i=4)
-                if a >= ON_VECTOR[u]:
-                    nc.vector.tensor_copy(out=dst, in_=src)
-                else:
-                    nc.scalar.copy(out=dst, in_=src)
+            for a, b, cut in LOADS[u]:
+                for lo, hi, copy in ((a, cut, nc.scalar.copy), (cut, b, nc.vector.tensor_copy)):
+                    if lo < hi:
+                        copy(out=pairs[u][:, 2 * lo : 2 * hi].rearrange("p (c i e) -> p c e i", i=4, e=2),
+                             in_=x_raw[u, a][:, :, lo - a : hi - a].rearrange("p e (c i) -> p c e i", i=4))
 
         def entries(c, n=1):
             return offsets[:, c * LIST_COLS : (c + n) * LIST_COLS]
@@ -116,6 +107,13 @@ def tile_picked_modgate_mlpsilu_l_kernel(tc, xT, gate, w1, w2_words, w2_scales, 
         round_pairs(0)
         pick_first(0)
         pick(0, 1, 3)
+
+        w1_at = LOADS[1][0][2]
+        w1_bf = tables[1][:, w1_at : w1_at + PACK * H // 2].bitcast(BF16)
+        nc.scalar.copy(out=w1_bf.rearrange("p (t m j) -> p m j t", t=PACK, j=PACK), in_=w1_raw[:].rearrange("p j (m t) -> p m j t", t=PACK))
+        w1_codes = keep.tile([P, H], U32, name="w1_codes", align_bytes=64)
+        w1_plane = keep.tile([P, H], U8, name="w1_plane", align_bytes=64)
+        nc.vector.quantize_mx(out=w1_codes[:].bitcast(FP8X4), scales=w1_plane[:], in_=w1_bf)
         round_pairs(1)
 
         y = [keep.tile([P, S], F32, name=f"y{r}") for r in range(2)]

@@ -13,6 +13,7 @@ U16 = mybir.dt.uint16
 U8 = mybir.dt.uint8
 FP8X4 = mybir.dt.float8_e4m3fn_x4
 MULT = mybir.AluOpType.mult
+ADD = mybir.AluOpType.add
 SILU = mybir.ActivationFunctionType.Silu
 
 P = 128
@@ -21,8 +22,8 @@ CHUNK = 256
 CHUNKS = S // CHUNK
 HALF = 128
 LIST_COLS = CHUNK // 16
-LOADS = (((0, 1024, 0), (1024, 2048, 2048)),
-         ((0, 1024, 896), (1024, 1664, 1024), (1664, 2048, 1664)))
+LOADS = (((0, 1024, 0), (1024, 2048, 1600)),
+         ((0, 1024, 800), (1024, 1664, 1024), (1664, 2048, 1792)))
 
 
 def tile_picked_modgate_mlpsilu_l_kernel(tc, xT, gate, w1, w2_words, w2_scales, offs, out):
@@ -31,26 +32,28 @@ def tile_picked_modgate_mlpsilu_l_kernel(tc, xT, gate, w1, w2_words, w2_scales, 
         keep = ctx.enter_context(tc.tile_pool(name="keep", bufs=1))
         psum = ctx.enter_context(tc.psum_pool(name="psum", bufs=1))
 
-        tables = [keep.tile([P, T], F32, name=f"table{u}", align_bytes=64) for u in range(2)]
-        pairs = [table[:].bitcast(BF16) for table in tables]
-        gate_table = tables[1][:]
-        gate_cols = tables[0][:, T - 16 :]
+        second_at = LOADS[0][1][2]
+        tables = keep.tile([P, second_at + T], F32, name="tables", align_bytes=64)
+        pairs = [tables[:, :T].bitcast(BF16), tables[:, second_at:].bitcast(BF16)]
+        gate_table = tables[:, second_at:]
+        gate_cols = tables[:, second_at - 16 : second_at]
         nc.sync.dma_start(out=gate_cols, in_=gate[0].rearrange("(p m) -> p m", m=16))
-        offsets = keep.tile([P, S // 16], U16, name="offsets")
-        nc.sync.dma_start(offsets[:], offs)
         x_rows = xT.rearrange("(p t) c -> p t c", t=PACK)
         x_raw = {}
 
-        def load_pair(u):
-            for a, b, cut in LOADS[u]:
-                raw = keep.tile([P, 2, b - a], F32, name=f"x_raw{u}_{a}")
-                nc.sync.dma_start(out=raw[:], in_=x_rows[:, 2 * u : 2 * u + 2, a:b])
-                x_raw[u, a] = raw
+        def load(u, a, b):
+            raw = keep.tile([P, 2, b - a], F32, name=f"x_raw{u}_{a}")
+            nc.sync.dma_start(out=raw[:], in_=x_rows[:, 2 * u : 2 * u + 2, a:b])
+            x_raw[u, a] = raw
 
-        load_pair(0)
+        load(0, *LOADS[0][0][:2])
+        offsets = keep.tile([P, S // 16], U16, name="offsets")
+        nc.sync.dma_start(offsets[:], offs)
+        load(0, *LOADS[0][1][:2])
         w1_raw = keep.tile([P, PACK, H], F32, name="w1_raw")
         nc.sync.dma_start(out=w1_raw[:], in_=w1.rearrange("(p j) c -> p j c", j=PACK))
-        load_pair(1)
+        for a, b, cut in LOADS[1]:
+            load(1, a, b)
         w2_codes = keep.tile([P, N], U32, name="w2_codes", align_bytes=64)
         nc.sync.dma_start(out=w2_codes[:].bitcast(I32), in_=w2_words[0].rearrange("p n t -> p (n t)").bitcast(I32))
         w2_plane = keep.tile([P, N], U8, name="w2_plane", align_bytes=64)
@@ -83,9 +86,10 @@ def tile_picked_modgate_mlpsilu_l_kernel(tc, xT, gate, w1, w2_words, w2_scales, 
         gate_picked = keep.tile([P, S], F32, name="gate_picked")
         nc.vector.tensor_copy(out=gate_picked[:], in_=gate_table.indirect(offsets[:]))
 
-        staged = keep.tile([P, 6 * CHUNK], U32, name="staged", align_bytes=64)
-        REST = S - CHUNK
-        first_words = staged[:, REST + CHUNK :]
+        slots = keep.tile([P, 5, CHUNK], U32, name="slots", align_bytes=64)
+        second = keep.tile([P, 2, CHUNK], U32, name="second", align_bytes=64)
+        woven = {0: slots[:, 2:4, :], 2: slots[:, 1:5:3, :]}
+        apart = {1: second[:], 3: slots[:, 0:4:3, :]}
 
         def round_pairs(u):
             for a, b, cut in LOADS[u]:
@@ -97,19 +101,16 @@ def tile_picked_modgate_mlpsilu_l_kernel(tc, xT, gate, w1, w2_words, w2_scales, 
         def entries(c, n=1):
             return offsets[:, c * LIST_COLS : (c + n) * LIST_COLS]
 
-        def pick_first(u):
-            nc.vector.tensor_copy(out=first_words.rearrange("p (s u) -> p s u", u=2)[:, :, u], in_=pairs[u].bitcast(U32).indirect(entries(0)))
-
-        def pick(u, c, n):
-            start = u * REST + (c - 1) * CHUNK
-            nc.vector.tensor_copy(out=staged[:, start : start + n * CHUNK], in_=pairs[u].bitcast(U32).indirect(entries(c, n)))
+        def pick(u, c):
+            dst = woven[c].rearrange("p g (s u) -> p g s u", u=2)[:, :, :, u] if c in woven else apart[c][:, u, :]
+            nc.vector.tensor_copy(out=dst, in_=pairs[u].bitcast(U32).indirect(entries(c)))
 
         round_pairs(0)
-        pick_first(0)
-        pick(0, 1, 3)
+        for c in range(CHUNKS):
+            pick(0, c)
 
-        w1_at = LOADS[1][0][2]
-        w1_bf = tables[1][:, w1_at : w1_at + PACK * H // 2].bitcast(BF16)
+        w1_at = second_at + LOADS[1][0][2]
+        w1_bf = tables[:, w1_at : w1_at + PACK * H // 2].bitcast(BF16)
         nc.scalar.copy(out=w1_bf.rearrange("p (t m j) -> p m j t", t=PACK, j=PACK), in_=w1_raw[:].rearrange("p j (m t) -> p m j t", t=PACK))
         w1_codes = keep.tile([P, H], U32, name="w1_codes", align_bytes=64)
         w1_plane = keep.tile([P, H], U8, name="w1_plane", align_bytes=64)
@@ -117,14 +118,28 @@ def tile_picked_modgate_mlpsilu_l_kernel(tc, xT, gate, w1, w2_words, w2_scales, 
         round_pairs(1)
 
         y = [keep.tile([P, S], F32, name=f"y{r}") for r in range(2)]
-        x_codes = [keep.tile([P, CHUNK], U32, name=f"x_codes{c}", align_bytes=64) for c in range(CHUNKS)]
+        x_codes = [keep.tile([P, CHUNK], U32, name=f"x_codes{c}", align_bytes=64) for c in range(2)]
         x_plane = [keep.tile([P, CHUNK], U8, name=f"x_plane{c}", align_bytes=64) for c in range(CHUNKS)]
-        h_bf = [keep.tile([P, PACK * CHUNK], BF16, name=f"h_bf{c}", align_bytes=64) for c in range(CHUNKS)]
+        h_bf = {c: keep.tile([P, PACK * CHUNK], BF16, name=f"h_bf{c}", align_bytes=64) for c in range(1, CHUNKS)}
+        h_first = [keep.tile([P, PACK * HALF], BF16, name=f"h_first{g}", align_bytes=64) for g in range(2)]
         h_codes = [keep.tile([P, CHUNK], U32, name=f"h_codes{c}", align_bytes=64) for c in range(CHUNKS)]
         h_plane = [keep.tile([P, CHUNK], U8, name=f"h_plane{c}", align_bytes=64) for c in range(CHUNKS)]
 
         def quantize(codes, plane, values, a, b):
             nc.vector.quantize_mx(out=codes[:, a:b].bitcast(FP8X4), scales=plane[:, a:b], in_=values[:, PACK * a : PACK * b])
+
+        def quantize_first(g):
+            cols = slice(g * HALF, (g + 1) * HALF)
+            nc.vector.quantize_mx(out=h_codes[0][:, cols].bitcast(FP8X4), scales=h_plane[0][:, cols], in_=h_first[g][:])
+
+        def quantize_woven(c, g):
+            cols = slice(g * HALF, (g + 1) * HALF)
+            nc.vector.quantize_mx(out=x_codes[c][:, cols].bitcast(FP8X4), scales=x_plane[c][:, cols], in_=woven[c][:, g, :].bitcast(BF16))
+
+        def weave(c, picked):
+            nc.scalar.copy(out=picked[:].bitcast(U32).rearrange("p (s i u) -> p s u i", i=4, u=2),
+                           in_=apart[c].rearrange("p u (s i) -> p s u i", i=4))
+            quantize(x_codes[c], x_plane[c], picked, 0, CHUNK)
 
         def hidden(c, g, tag):
             cols = slice(g * HALF, (g + 1) * HALF)
@@ -133,7 +148,8 @@ def tile_picked_modgate_mlpsilu_l_kernel(tc, xT, gate, w1, w2_words, w2_scales, 
                 chans = slice(t * P, (t + 1) * P)
                 nc.tensor.matmul_mx(out=bank[:, t, :], lhsT=w1_codes[:, chans].bitcast(FP8X4), lhsT_scale=w1_plane[:, chans],
                                     rhs=x_codes[c][:, cols].bitcast(FP8X4), rhs_scale=x_plane[c][:, cols], start=True, stop=True)
-            dst = h_bf[c][:, g * PACK * HALF : (g + 1) * PACK * HALF].rearrange("p (n t) -> p n t", t=PACK)
+            values = h_first[g][:] if c == 0 else h_bf[c][:, g * PACK * HALF : (g + 1) * PACK * HALF]
+            dst = values.rearrange("p (n t) -> p n t", t=PACK)
             nc.scalar.activation(out=dst, in_=bank[:].rearrange("p t n -> p n t"), func=SILU)
 
         def result(dst, r, c, a, b):
@@ -141,60 +157,62 @@ def tile_picked_modgate_mlpsilu_l_kernel(tc, xT, gate, w1, w2_words, w2_scales, 
             nc.tensor.matmul_mx(out=dst, lhsT=w2_codes[:, rows].bitcast(FP8X4), lhsT_scale=w2_plane[:, rows],
                                 rhs=h_codes[c][:, a:b].bitcast(FP8X4), rhs_scale=h_plane[c][:, a:b], start=True, stop=True)
 
-        def place(r, c, n=1):
-            cols = slice(c * CHUNK, (c + n) * CHUNK)
-            nc.vector.tensor_tensor(placed[r][:].indirect(entries(c, n)), y[r][:, cols], gate_picked[:, cols], MULT)
+        def place(r, a, b):
+            nc.vector.tensor_tensor(placed[r][:].indirect(offsets[:, a // 16 : b // 16]), y[r][:, a:b], gate_picked[:, a:b], MULT)
 
-        halves = staged[:].rearrange("p (u s i) -> p s u i", u=2, i=4)
+        def empty(bank, r, a, b):
+            nc.scalar.copy(out=y[r][:, a:b], in_=bank)
 
-        def weave(c, picked):
-            a, b = (c - 1) * CHUNK, c * CHUNK
-            nc.scalar.copy(out=picked.bitcast(U32).rearrange("p (s i u) -> p s u i", i=4, u=2), in_=halves[:, a // 4 : b // 4])
-            quantize(x_codes[c], x_plane[c], picked, 0, CHUNK)
-
-        def empty(bank, r, c, n=1):
-            nc.scalar.copy(out=y[r][:, c * CHUNK : (c + n) * CHUNK], in_=bank)
-
-        def held(r, c, tag):
-            bank = psum.tile([P, CHUNK], F32, name=f"y_bank{r}_{c}", tag=tag)
-            result(bank[:], r, c, 0, CHUNK)
-            empty(bank[:], r, c)
-            place(r, c)
-
-        pick_first(1)
-        pick(1, 1, 1)
-        y_first = psum.tile([P, CHUNK], F32, name="y_first", tag="bank4")
-        for g in range(2):
-            quantize(x_codes[0], x_plane[0], first_words.bitcast(BF16), g * HALF, (g + 1) * HALF)
-        picked_second = keep.tile([P, PACK * CHUNK], BF16, name="picked_second", align_bytes=64)
-        weave(1, picked_second[:])
-        pick(1, 2, 2)
-        for g in range(2):
-            hidden(0, g, f"bank{g}")
-            quantize(h_codes[0], h_plane[0], h_bf[0], g * HALF, (g + 1) * HALF)
-            result(y_first[:, g * HALF : (g + 1) * HALF], 0, 0, g * HALF, (g + 1) * HALF)
-
-        picked_rest = keep.tile([P, 2 * PACK * CHUNK], BF16, name="picked_rest", tag="x_codes0", align_bytes=64)
-        weave(2, picked_rest[:, : PACK * CHUNK])
-        weave(3, picked_rest[:, PACK * CHUNK :])
-        empty(y_first[:], 0, 0)
-        place(0, 0)
-        hidden(1, 0, "bank2")
-        hidden(1, 1, "bank3")
+        pick(1, 0)
+        pick(1, 1)
+        quantize_woven(0, 0)
+        quantize_woven(0, 1)
+        pick(1, 2)
+        picked1 = keep.tile([P, PACK * CHUNK], BF16, name="picked1", align_bytes=64)
+        weave(1, picked1)
+        pick(1, 3)
+        y_first = psum.tile([P, HALF], F32, name="y_first", tag="bank4")
+        y_second = psum.tile([P, CHUNK + HALF], F32, name="y_second", tag="bank5")
+        hidden(0, 0, "bank0")
+        quantize_first(0)
+        result(y_first[:], 0, 0, 0, HALF)
+        x_codes.append(keep.tile([P, CHUNK], U32, name="x_codes2", tag="h_first0", align_bytes=64))
+        quantize_woven(2, 0)
+        quantize_woven(2, 1)
+        hidden(0, 1, "bank1")
+        quantize_first(1)
+        weighted = keep.tile([P, HALF], F32, name="weighted")
+        nc.vector.tensor_tensor(weighted[:], y_first[:], gate_picked[:, :HALF], MULT)
+        x_codes.append(keep.tile([P, CHUNK], U32, name="x_codes3", tag="h_first1", align_bytes=64))
+        picked3 = keep.tile([P, PACK * CHUNK], BF16, name="picked3", tag="x_codes0", align_bytes=64)
+        weave(3, picked3)
+        nc.vector.tensor_tensor(placed[0][:].indirect(offsets[:, : HALF // 16]), weighted[:], placed[1][:, :HALF], ADD)
+        result(y_second[:, :CHUNK], 1, 0, 0, CHUNK)
+        result(y_second[:, CHUNK:], 0, 0, HALF, CHUNK)
+        hidden(1, 0, "bank0")
+        hidden(1, 1, "bank1")
         quantize(h_codes[1], h_plane[1], h_bf[1], 0, CHUNK)
+        empty(y_second[:, :CHUNK], 1, 0, CHUNK)
+        place(1, 0, CHUNK)
+        empty(y_second[:, CHUNK:], 0, HALF, CHUNK)
+        y_third = psum.tile([P, CHUNK], F32, name="y_third", tag="bank4")
+        result(y_third[:], 0, 1, 0, CHUNK)
+        empty(y_third[:], 0, CHUNK, 2 * CHUNK)
+        place(0, HALF, 2 * CHUNK)
         hidden(2, 0, "bank0")
-        held(1, 0, "bank3")
         hidden(2, 1, "bank1")
         quantize(h_codes[2], h_plane[2], h_bf[2], 0, CHUNK)
-        hidden(3, 0, "bank5")
-        held(0, 1, "bank1")
-        hidden(3, 1, "bank4")
+        hidden(3, 0, "bank0")
+        hidden(3, 1, "bank1")
         quantize(h_codes[3], h_plane[3], h_bf[3], 0, CHUNK)
-        held(1, 1, "bank4")
+        y_fourth = psum.tile([P, CHUNK], F32, name="y_fourth", tag="bank1")
+        result(y_fourth[:], 1, 1, 0, CHUNK)
+        empty(y_fourth[:], 1, CHUNK, 2 * CHUNK)
+        place(1, CHUNK, 2 * CHUNK)
         for r in range(2):
             y_last = psum.tile([P, 2, CHUNK], F32, name=f"y_last{r}", tag=f"bank{6 + r}")
             for c in (2, 3):
                 result(y_last[:, c - 2, :], r, c, 0, CHUNK)
-            empty(y_last[:].rearrange("p c s -> p (c s)"), r, 2, 2)
-            place(r, 2, 2)
+            empty(y_last[:].rearrange("p c s -> p (c s)"), r, 2 * CHUNK, S)
+            place(r, 2 * CHUNK, S)
             nc.sync.dma_start(out=out[r * P : (r + 1) * P, :], in_=placed[r][:])

@@ -13,50 +13,39 @@ U16 = mybir.dt.uint16
 U8 = mybir.dt.uint8
 FP8X4 = mybir.dt.float8_e4m3fn_x4
 MULT = mybir.AluOpType.mult
-ADD = mybir.AluOpType.add
 SILU = mybir.ActivationFunctionType.Silu
+COPY = mybir.ActivationFunctionType.Copy
 
 P = 128
 PACK = 4
 CHUNK = 256
 CHUNKS = S // CHUNK
 HALF = 128
-LIST_COLS = CHUNK // 16
-LOADS = (((0, 1024, 0), (1024, 2048, 1600)),
-         ((0, 1024, 800), (1024, 1664, 1024), (1664, 2048, 1792)))
+W1_CUT = 80
+PIECES = ((0, 128), (128, 384), (384, 640), (640, 768), (768, 1024))
 
 
 def tile_picked_modgate_mlpsilu_l_kernel(tc, xT, gate, w1, w2_words, w2_scales, offs, out):
     nc = tc.nc
     with ExitStack() as ctx:
         keep = ctx.enter_context(tc.tile_pool(name="keep", bufs=1))
+        shared = ctx.enter_context(tc.tile_pool(name="shared", bufs=1))
         psum = ctx.enter_context(tc.psum_pool(name="psum", bufs=1))
 
-        second_at = LOADS[0][1][2]
-        tables = keep.tile([P, second_at + T], F32, name="tables", align_bytes=64)
-        pairs = [tables[:, :T].bitcast(BF16), tables[:, second_at:].bitcast(BF16)]
-        gate_table = tables[:, second_at:]
-        gate_cols = tables[:, second_at - 16 : second_at]
-        nc.sync.dma_start(out=gate_cols, in_=gate[0].rearrange("(p m) -> p m", m=16))
+        gate_cols = shared.tile([P, 336], F32, name="gate_cols", offset=8192 - 32)
+        nc.sync.dma_start(out=gate_cols[:, :16], in_=gate[0].rearrange("(p m) -> p m", m=16))
         x_rows = xT.rearrange("(p t) c -> p t c", t=PACK)
-        x_raw = {}
-
-        def load(u, a, b):
-            raw = keep.tile([P, 2, b - a], F32, name=f"x_raw{u}_{a}")
-            nc.sync.dma_start(out=raw[:], in_=x_rows[:, 2 * u : 2 * u + 2, a:b])
-            x_raw[u, a] = raw
-
-        load(0, *LOADS[0][0][:2])
+        x_plane_raw = [keep.tile([P, T], F32, name=f"x_raw{t}") for t in range(PACK)]
+        nc.sync.dma_start(out=x_plane_raw[0][:], in_=x_rows[:, 0, :])
         offsets = keep.tile([P, S // 16], U16, name="offsets")
         nc.sync.dma_start(offsets[:], offs)
-        load(0, *LOADS[0][1][:2])
-        w1_raw = keep.tile([P, PACK, H], F32, name="w1_raw")
+        for t in range(1, PACK):
+            nc.sync.dma_start(out=x_plane_raw[t][:], in_=x_rows[:, t, :])
+        w1_raw = shared.tile([P, PACK, H], F32, name="w1_raw", offset=9472)
         nc.sync.dma_start(out=w1_raw[:], in_=w1.rearrange("(p j) c -> p j c", j=PACK))
-        for a, b, cut in LOADS[1]:
-            load(1, a, b)
-        w2_codes = keep.tile([P, N], U32, name="w2_codes", align_bytes=64)
+        w2_codes = shared.tile([P, N], U32, name="w2_codes", align_bytes=64, offset=8192)
         nc.sync.dma_start(out=w2_codes[:].bitcast(I32), in_=w2_words[0].rearrange("p n t -> p (n t)").bitcast(I32))
-        w2_plane = keep.tile([P, N], U8, name="w2_plane", align_bytes=64)
+        w2_plane = shared.tile([P, N], U8, name="w2_plane", align_bytes=64, offset=9216)
         nc.vector.memset(w2_plane[:].bitcast(U32), 0)
         for q in range(4):
             nc.sync.dma_start(out=w2_plane[32 * q : 32 * q + 4, :].bitcast(I32), in_=w2_scales[0, 4 * q : 4 * q + 4, :].bitcast(I32))
@@ -66,153 +55,153 @@ def tile_picked_modgate_mlpsilu_l_kernel(tc, xT, gate, w1, w2_words, w2_scales, 
         nc.vector.memset(warm[:], 0.0)
         nc.scalar.activation(out=warm_out[:], in_=warm[:], func=SILU)
         identity = keep.tile([P, P], F32, name="identity", align_bytes=64)
-        zeros = keep.tile([P, P], F32, name="zeros", tag="placed1")
+        zeros = keep.tile([P, P], F32, name="zeros")
         nc.gpsimd.memset(zeros[:], 0.0)
         nc.gpsimd.affine_select(out=identity[:], in_=zeros[:], compare_op=mybir.AluOpType.not_equal, fill=1.0, base=0,
                                 pattern=[[-1, P]], channel_multiplier=1)
 
         placed = [keep.tile([P, T], F32, name=f"placed{r}") for r in range(2)]
-        nc.vector.memset(placed[0][:].bitcast(I32), 0)
-        nc.gpsimd.memset(placed[1][:].bitcast(I32), 0)
+        for r in range(2):
+            nc.vector.memset(placed[r][:].bitcast(I32), 0)
 
+        def entries(a, b):
+            return offsets[:, a // 16 : b // 16]
+
+        gate_table = keep.tile([P, T], F32, name="gate_table")
         for a in range(4):
             bank = psum.tile([P, 4, P], F32, name=f"gate_bank{a}", tag=f"bank{a}")
             for b in range(4):
                 m = 4 * a + b
                 nc.tensor.transpose(bank[:, b, :], gate_cols[:, m : m + 1].to_broadcast([P, P]), identity[:])
-            dst = gate_table.rearrange("p (n a b) -> p a n b", a=4, b=4)[:, a]
+            dst = gate_table[:].rearrange("p (n a b) -> p a n b", a=4, b=4)[:, a]
             nc.scalar.copy(out=dst, in_=bank[:].rearrange("p b n -> p n b"))
+        scores = keep.tile([P, S], F32, name="scores")
+        nc.scalar.activation(out=scores[:], in_=gate_table[:].indirect(offsets[:]), func=COPY)
 
-        gate_picked = keep.tile([P, S], F32, name="gate_picked")
-        nc.vector.tensor_copy(out=gate_picked[:], in_=gate_table.indirect(offsets[:]))
+        picked = shared.tile([P, PACK, S], BF16, name="picked", offset=0)
 
-        slots = keep.tile([P, 5, CHUNK], U32, name="slots", align_bytes=64)
-        second = keep.tile([P, 2, CHUNK], U32, name="second", align_bytes=64)
-        woven = {0: slots[:, 2:4, :], 2: slots[:, 1:5:3, :]}
-        apart = {1: second[:], 3: slots[:, 0:4:3, :]}
+        def pick_on_vector(t, a, b):
+            nc.vector.tensor_copy(out=picked[:, t, a:b], in_=x_plane_raw[t][:].indirect(entries(a, b)))
 
-        def round_pairs(u):
-            for a, b, cut in LOADS[u]:
-                for lo, hi, copy in ((a, cut, nc.scalar.copy), (cut, b, nc.vector.tensor_copy)):
-                    if lo < hi:
-                        copy(out=pairs[u][:, 2 * lo : 2 * hi].rearrange("p (c i e) -> p c e i", i=4, e=2),
-                             in_=x_raw[u, a][:, :, lo - a : hi - a].rearrange("p e (c i) -> p c e i", i=4))
+        def pick_on_scalar(t, a, b):
+            nc.scalar.activation(out=picked[:, t, a:b], in_=x_plane_raw[t][:].indirect(entries(a, b)), func=COPY)
 
-        def entries(c, n=1):
-            return offsets[:, c * LIST_COLS : (c + n) * LIST_COLS]
+        pick_on_vector(0, 0, S)
+        for t in (1, 2):
+            pick_on_vector(t, 0, S // 2)
+            pick_on_scalar(t, S // 2, S)
+        pick_on_vector(3, *PIECES[0])
+        pick_on_scalar(3, *PIECES[1])
+        pick_on_scalar(3, *PIECES[2])
+        pick_on_scalar(3, PIECES[3][0], S)
 
-        def pick(u, c):
-            dst = woven[c].rearrange("p g (s u) -> p g s u", u=2)[:, :, :, u] if c in woven else apart[c][:, u, :]
-            nc.vector.tensor_copy(out=dst, in_=pairs[u].bitcast(U32).indirect(entries(c)))
+        woven_at = (17664, 18688, 9472, 20736, 21760)
+        woven = [shared.tile([P, PACK * (b - a)], BF16, name=f"woven{i}", align_bytes=64, offset=woven_at[i]) for i, (a, b) in enumerate(PIECES)]
+        x_codes = [keep.tile([P, b - a], U32, name=f"x_codes{i}", align_bytes=64) for i, (a, b) in enumerate(PIECES)]
+        x_scales = [keep.tile([P, b - a], U8, name=f"x_scales{i}", align_bytes=64) for i, (a, b) in enumerate(PIECES)]
 
-        round_pairs(0)
-        for c in range(CHUNKS):
-            pick(0, c)
+        def weave(i, copy):
+            a, b = PIECES[i]
+            copy(out=woven[i][:].rearrange("p (s i t) -> p s t i", i=4, t=PACK),
+                 in_=picked[:, :, a:b].rearrange("p t (s i) -> p s t i", i=4))
 
-        w1_at = second_at + LOADS[1][0][2]
-        w1_bf = tables[:, w1_at : w1_at + PACK * H // 2].bitcast(BF16)
-        nc.scalar.copy(out=w1_bf.rearrange("p (t m j) -> p m j t", t=PACK, j=PACK), in_=w1_raw[:].rearrange("p j (m t) -> p m j t", t=PACK))
+        def quantize_x(i):
+            nc.vector.quantize_mx(out=x_codes[i][:].bitcast(FP8X4), scales=x_scales[i][:], in_=woven[i][:])
+
+        weave(0, nc.vector.tensor_copy)
+        weave(1, nc.vector.tensor_copy)
+        quantize_x(0)
+        quantize_x(1)
+
+        w1_bf = shared.tile([P, PACK * H], BF16, name="w1_bf", align_bytes=64, offset=20736)
+        dealt = w1_bf[:].rearrange("p (t m j) -> p m j t", t=PACK, j=PACK)
+        plain = w1_raw[:].rearrange("p j (m t) -> p m j t", t=PACK)
+        nc.vector.tensor_copy(out=dealt[:, :W1_CUT], in_=plain[:, :W1_CUT])
+        nc.scalar.copy(out=dealt[:, W1_CUT:], in_=plain[:, W1_CUT:])
         w1_codes = keep.tile([P, H], U32, name="w1_codes", align_bytes=64)
-        w1_plane = keep.tile([P, H], U8, name="w1_plane", align_bytes=64)
-        nc.vector.quantize_mx(out=w1_codes[:].bitcast(FP8X4), scales=w1_plane[:], in_=w1_bf)
-        round_pairs(1)
+        w1_scales = keep.tile([P, H], U8, name="w1_scales", align_bytes=64)
+        for t in range(PACK):
+            chans = slice(t * P, (t + 1) * P)
+            nc.vector.quantize_mx(out=w1_codes[:, chans].bitcast(FP8X4), scales=w1_scales[:, chans],
+                                  in_=w1_bf[:, t * PACK * P : (t + 1) * PACK * P])
 
-        y = [keep.tile([P, S], F32, name=f"y{r}") for r in range(2)]
-        x_codes = [keep.tile([P, CHUNK], U32, name=f"x_codes{c}", align_bytes=64) for c in range(2)]
-        x_plane = [keep.tile([P, CHUNK], U8, name=f"x_plane{c}", align_bytes=64) for c in range(CHUNKS)]
-        h_bf = {c: keep.tile([P, PACK * CHUNK], BF16, name=f"h_bf{c}", align_bytes=64) for c in range(1, CHUNKS)}
-        h_first = [keep.tile([P, PACK * HALF], BF16, name=f"h_first{g}", align_bytes=64) for g in range(2)]
         h_codes = [keep.tile([P, CHUNK], U32, name=f"h_codes{c}", align_bytes=64) for c in range(CHUNKS)]
-        h_plane = [keep.tile([P, CHUNK], U8, name=f"h_plane{c}", align_bytes=64) for c in range(CHUNKS)]
+        h_bf = [keep.tile([P, PACK * CHUNK], BF16, name=f"h_bf{c}", tag="h_codes0" if c == 2 else f"h_bf{c}", align_bytes=64) for c in range(CHUNKS)]
+        h_scales = [keep.tile([P, CHUNK], U8, name=f"h_scales{c}", align_bytes=64) for c in range(CHUNKS)]
 
-        def quantize(codes, plane, values, a, b):
-            nc.vector.quantize_mx(out=codes[:, a:b].bitcast(FP8X4), scales=plane[:, a:b], in_=values[:, PACK * a : PACK * b])
-
-        def quantize_first(g):
-            cols = slice(g * HALF, (g + 1) * HALF)
-            nc.vector.quantize_mx(out=h_codes[0][:, cols].bitcast(FP8X4), scales=h_plane[0][:, cols], in_=h_first[g][:])
-
-        def quantize_woven(c, g):
-            cols = slice(g * HALF, (g + 1) * HALF)
-            nc.vector.quantize_mx(out=x_codes[c][:, cols].bitcast(FP8X4), scales=x_plane[c][:, cols], in_=woven[c][:, g, :].bitcast(BF16))
-
-        def weave(c, picked):
-            nc.scalar.copy(out=picked[:].bitcast(U32).rearrange("p (s i u) -> p s u i", i=4, u=2),
-                           in_=apart[c].rearrange("p u (s i) -> p s u i", i=4))
-            quantize(x_codes[c], x_plane[c], picked, 0, CHUNK)
-
-        def hidden(c, g, tag):
-            cols = slice(g * HALF, (g + 1) * HALF)
-            bank = psum.tile([P, PACK, HALF], F32, name=f"h_bank{c}_{g}", tag=tag)
+        def hidden(g):
+            c, cols = g // 2, slice((g % 2) * HALF, (g % 2 + 1) * HALF)
+            i = [i for i, (a, b) in enumerate(PIECES) if a <= g * HALF < b][0]
+            tokens = slice(g * HALF - PIECES[i][0], (g + 1) * HALF - PIECES[i][0])
+            bank = psum.tile([P, PACK, HALF], F32, name=f"h_bank{g}", tag=f"bank{4 + g % 4}")
             for t in range(PACK):
                 chans = slice(t * P, (t + 1) * P)
-                nc.tensor.matmul_mx(out=bank[:, t, :], lhsT=w1_codes[:, chans].bitcast(FP8X4), lhsT_scale=w1_plane[:, chans],
-                                    rhs=x_codes[c][:, cols].bitcast(FP8X4), rhs_scale=x_plane[c][:, cols], start=True, stop=True)
-            values = h_first[g][:] if c == 0 else h_bf[c][:, g * PACK * HALF : (g + 1) * PACK * HALF]
-            dst = values.rearrange("p (n t) -> p n t", t=PACK)
-            nc.scalar.activation(out=dst, in_=bank[:].rearrange("p t n -> p n t"), func=SILU)
+                nc.tensor.matmul_mx(out=bank[:, t, :], lhsT=w1_codes[:, chans].bitcast(FP8X4), lhsT_scale=w1_scales[:, chans],
+                                    rhs=x_codes[i][:, tokens].bitcast(FP8X4), rhs_scale=x_scales[i][:, tokens], start=True, stop=True)
+            nc.scalar.activation(out=h_bf[c][:, PACK * cols.start : PACK * cols.stop].rearrange("p (n t) -> p n t", t=PACK), in_=bank[:].rearrange("p t n -> p n t"), func=SILU)
 
-        def result(dst, r, c, a, b):
+        def quantize_h(c, a, b):
+            nc.vector.quantize_mx(out=h_codes[c][:, a:b].bitcast(FP8X4), scales=h_scales[c][:, a:b], in_=h_bf[c][:, PACK * a : PACK * b])
+
+        def result(bank, r, c):
             rows = slice(r * P, (r + 1) * P)
-            nc.tensor.matmul_mx(out=dst, lhsT=w2_codes[:, rows].bitcast(FP8X4), lhsT_scale=w2_plane[:, rows],
-                                rhs=h_codes[c][:, a:b].bitcast(FP8X4), rhs_scale=h_plane[c][:, a:b], start=True, stop=True)
+            nc.tensor.matmul_mx(out=bank, lhsT=w2_codes[:, rows].bitcast(FP8X4), lhsT_scale=w2_plane[:, rows],
+                                rhs=h_codes[c][:].bitcast(FP8X4), rhs_scale=h_scales[c][:], start=True, stop=True)
 
-        def place(r, a, b):
-            nc.vector.tensor_tensor(placed[r][:].indirect(offsets[:, a // 16 : b // 16]), y[r][:, a:b], gate_picked[:, a:b], MULT)
+        def place_on_scalar(values, c):
+            nc.scalar.activation(out=placed[1][:].indirect(entries(c * CHUNK, (c + 1) * CHUNK)), in_=values, func=COPY)
 
-        def empty(bank, r, a, b):
-            nc.scalar.copy(out=y[r][:, a:b], in_=bank)
+        weave(2, nc.scalar.copy)
+        weave(3, nc.vector.tensor_copy)
+        quantize_x(2)
+        weave(4, nc.vector.tensor_copy)
+        hidden(0)
+        hidden(1)
+        hidden(2)
+        hidden(3)
+        quantize_h(0, 0, HALF)
+        quantize_h(0, HALF, CHUNK)
+        plain_banks = ("bank6", "bank7", "bank6", "bank5")
+        y_plain = [keep.tile([P, CHUNK], F32, name=f"y_plain{c}") for c in range(CHUNKS)]
 
-        pick(1, 0)
-        pick(1, 1)
-        quantize_woven(0, 0)
-        quantize_woven(0, 1)
-        pick(1, 2)
-        picked1 = keep.tile([P, PACK * CHUNK], BF16, name="picked1", align_bytes=64)
-        weave(1, picked1)
-        pick(1, 3)
-        y_first = psum.tile([P, HALF], F32, name="y_first", tag="bank4")
-        y_second = psum.tile([P, CHUNK + HALF], F32, name="y_second", tag="bank5")
-        hidden(0, 0, "bank0")
-        quantize_first(0)
-        result(y_first[:], 0, 0, 0, HALF)
-        x_codes.append(keep.tile([P, CHUNK], U32, name="x_codes2", tag="h_first0", align_bytes=64))
-        quantize_woven(2, 0)
-        quantize_woven(2, 1)
-        hidden(0, 1, "bank1")
-        quantize_first(1)
-        weighted = keep.tile([P, HALF], F32, name="weighted")
-        nc.vector.tensor_tensor(weighted[:], y_first[:], gate_picked[:, :HALF], MULT)
-        x_codes.append(keep.tile([P, CHUNK], U32, name="x_codes3", tag="h_first1", align_bytes=64))
-        picked3 = keep.tile([P, PACK * CHUNK], BF16, name="picked3", tag="x_codes0", align_bytes=64)
-        weave(3, picked3)
-        nc.vector.tensor_tensor(placed[0][:].indirect(offsets[:, : HALF // 16]), weighted[:], placed[1][:, :HALF], ADD)
-        result(y_second[:, :CHUNK], 1, 0, 0, CHUNK)
-        result(y_second[:, CHUNK:], 0, 0, HALF, CHUNK)
-        hidden(1, 0, "bank0")
-        hidden(1, 1, "bank1")
-        quantize(h_codes[1], h_plane[1], h_bf[1], 0, CHUNK)
-        empty(y_second[:, :CHUNK], 1, 0, CHUNK)
-        place(1, 0, CHUNK)
-        empty(y_second[:, CHUNK:], 0, HALF, CHUNK)
-        y_third = psum.tile([P, CHUNK], F32, name="y_third", tag="bank4")
-        result(y_third[:], 0, 1, 0, CHUNK)
-        empty(y_third[:], 0, CHUNK, 2 * CHUNK)
-        place(0, HALF, 2 * CHUNK)
-        hidden(2, 0, "bank0")
-        hidden(2, 1, "bank1")
-        quantize(h_codes[2], h_plane[2], h_bf[2], 0, CHUNK)
-        hidden(3, 0, "bank0")
-        hidden(3, 1, "bank1")
-        quantize(h_codes[3], h_plane[3], h_bf[3], 0, CHUNK)
-        y_fourth = psum.tile([P, CHUNK], F32, name="y_fourth", tag="bank1")
-        result(y_fourth[:], 1, 1, 0, CHUNK)
-        empty(y_fourth[:], 1, CHUNK, 2 * CHUNK)
-        place(1, CHUNK, 2 * CHUNK)
-        for r in range(2):
-            y_last = psum.tile([P, 2, CHUNK], F32, name=f"y_last{r}", tag=f"bank{6 + r}")
-            for c in (2, 3):
-                result(y_last[:, c - 2, :], r, c, 0, CHUNK)
-            empty(y_last[:].rearrange("p c s -> p (c s)"), r, 2 * CHUNK, S)
-            place(r, 2 * CHUNK, S)
-            nc.sync.dma_start(out=out[r * P : (r + 1) * P, :], in_=placed[r][:])
+        def empty(c):
+            bank = psum.tile([P, CHUNK], F32, name=f"y_low{c}", tag=plain_banks[c])
+            result(bank[:], 0, c)
+            nc.scalar.copy(out=y_plain[c][:], in_=bank[:])
+
+        def place_on_vector(c, scores):
+            nc.vector.tensor_tensor(placed[0][:].indirect(entries(c * CHUNK, (c + 1) * CHUNK)), y_plain[c][:], scores, MULT)
+
+        empty(0)
+        high_first = psum.tile([P, CHUNK], F32, name="y_high0", tag="bank0")
+        result(high_first[:], 1, 0)
+        quantize_x(3)
+        quantize_x(4)
+        weighted0 = keep.tile([P, CHUNK], F32, name="weighted0")
+        nc.vector.tensor_tensor(weighted0[:], high_first[:], scores[:, :CHUNK], MULT)
+        quantize_h(1, 0, CHUNK)
+        place_on_vector(0, scores[:, :CHUNK])
+        for g in range(4, 2 * CHUNKS):
+            hidden(g)
+        high_middle = psum.tile([P, 2, CHUNK], F32, name="y_high12", tag="bank1")
+        high_last = psum.tile([P, CHUNK], F32, name="y_high3", tag="bank2")
+        result(high_middle[:, 0, :], 1, 1)
+        empty(1)
+        quantize_h(2, 0, CHUNK)
+        empty(2)
+        result(high_middle[:, 1, :], 1, 2)
+        quantize_h(3, 0, CHUNK)
+        empty(3)
+        result(high_last[:], 1, 3)
+        weighted_middle = keep.tile([P, 2 * CHUNK], F32, name="weighted_middle")
+        nc.vector.tensor_tensor(weighted_middle[:], high_middle[:].rearrange("p c s -> p (c s)"), scores[:, CHUNK : 3 * CHUNK], MULT)
+        for c in range(1, CHUNKS):
+            place_on_vector(c, scores[:, c * CHUNK : (c + 1) * CHUNK])
+        nc.sync.dma_start(out=out[:P, :], in_=placed[0][:])
+        weighted_last = keep.tile([P, CHUNK], F32, name="weighted_last", tag="y_plain3")
+        nc.vector.tensor_tensor(weighted_last[:], high_last[:], scores[:, 3 * CHUNK :], MULT)
+        place_on_scalar(weighted_middle[:, :CHUNK], 1)
+        place_on_scalar(weighted0[:], 0)
+        place_on_scalar(weighted_middle[:, CHUNK:], 2)
+        place_on_scalar(weighted_last[:], 3)
+        nc.sync.dma_start(out=out[P:, :], in_=placed[1][:])

@@ -13,16 +13,16 @@ U16 = mybir.dt.uint16
 U8 = mybir.dt.uint8
 FP8X4 = mybir.dt.float8_e4m3fn_x4
 MULT = mybir.AluOpType.mult
+ADD = mybir.AluOpType.add
 SILU = mybir.ActivationFunctionType.Silu
 COPY = mybir.ActivationFunctionType.Copy
 
 P = 128
 PACK = 4
-CHUNK = 256
-CHUNKS = S // CHUNK
-HALF = 128
+GROUP = 128
 W1_CUT = 80
 PIECES = ((0, 128), (128, 384), (384, 640), (640, 768), (768, 1024))
+RUNS = PIECES
 
 
 def tile_picked_modgate_mlpsilu_l_kernel(tc, xT, gate, w1, w2_words, w2_scales, offs, out):
@@ -86,10 +86,11 @@ def tile_picked_modgate_mlpsilu_l_kernel(tc, xT, gate, w1, w2_words, w2_scales, 
         def pick_on_scalar(t, a, b):
             nc.scalar.activation(out=picked[:, t, a:b], in_=x_plane_raw[t][:].indirect(entries(a, b)), func=COPY)
 
-        pick_on_vector(0, 0, S)
-        for t in (1, 2):
-            pick_on_vector(t, 0, S // 2)
-            pick_on_scalar(t, S // 2, S)
+        pick_on_vector(0, 0, S // 2)
+        pick_on_scalar(0, S // 2, S)
+        pick_on_vector(1, 0, S)
+        pick_on_vector(2, 0, S // 2)
+        pick_on_scalar(2, S // 2, S)
         pick_on_vector(3, *PIECES[0])
         pick_on_scalar(3, *PIECES[1])
         pick_on_scalar(3, *PIECES[2])
@@ -125,83 +126,95 @@ def tile_picked_modgate_mlpsilu_l_kernel(tc, xT, gate, w1, w2_words, w2_scales, 
             nc.vector.quantize_mx(out=w1_codes[:, chans].bitcast(FP8X4), scales=w1_scales[:, chans],
                                   in_=w1_bf[:, t * PACK * P : (t + 1) * PACK * P])
 
-        h_codes = [keep.tile([P, CHUNK], U32, name=f"h_codes{c}", align_bytes=64) for c in range(CHUNKS)]
-        h_bf = [keep.tile([P, PACK * CHUNK], BF16, name=f"h_bf{c}", tag="h_codes0" if c == 2 else f"h_bf{c}", align_bytes=64) for c in range(CHUNKS)]
-        h_scales = [keep.tile([P, CHUNK], U8, name=f"h_scales{c}", align_bytes=64) for c in range(CHUNKS)]
+        h_codes = [keep.tile([P, b - a], U32, name=f"h_codes{i}", align_bytes=64) for i, (a, b) in enumerate(RUNS)]
+        h_scales = [keep.tile([P, b - a], U8, name=f"h_scales{i}", align_bytes=64) for i, (a, b) in enumerate(RUNS)]
+        h_bf = [keep.tile([P, PACK * (b - a)], BF16, name=f"h_bf{i}", tag="h_codes1" if i == 4 else f"h_bf{i}", align_bytes=64)
+                for i, (a, b) in enumerate(RUNS)]
 
         def hidden(g):
-            c, cols = g // 2, slice((g % 2) * HALF, (g % 2 + 1) * HALF)
-            i = [i for i, (a, b) in enumerate(PIECES) if a <= g * HALF < b][0]
-            tokens = slice(g * HALF - PIECES[i][0], (g + 1) * HALF - PIECES[i][0])
-            bank = psum.tile([P, PACK, HALF], F32, name=f"h_bank{g}", tag=f"bank{4 + g % 4}")
+            a = g * GROUP
+            i = [i for i, (lo, hi) in enumerate(PIECES) if lo <= a < hi][0]
+            tokens = slice(a - PIECES[i][0], a + GROUP - PIECES[i][0])
+            bank = psum.tile([P, PACK, GROUP], F32, name=f"h_bank{g}", tag=f"bank{4 + g % 4}")
             for t in range(PACK):
                 chans = slice(t * P, (t + 1) * P)
                 nc.tensor.matmul_mx(out=bank[:, t, :], lhsT=w1_codes[:, chans].bitcast(FP8X4), lhsT_scale=w1_scales[:, chans],
                                     rhs=x_codes[i][:, tokens].bitcast(FP8X4), rhs_scale=x_scales[i][:, tokens], start=True, stop=True)
-            nc.scalar.activation(out=h_bf[c][:, PACK * cols.start : PACK * cols.stop].rearrange("p (n t) -> p n t", t=PACK), in_=bank[:].rearrange("p t n -> p n t"), func=SILU)
+            values = h_bf[i][:, PACK * tokens.start : PACK * tokens.stop]
+            nc.scalar.activation(out=values.rearrange("p (n t) -> p n t", t=PACK), in_=bank[:].rearrange("p t n -> p n t"), func=SILU)
 
-        def quantize_h(c, a, b):
-            nc.vector.quantize_mx(out=h_codes[c][:, a:b].bitcast(FP8X4), scales=h_scales[c][:, a:b], in_=h_bf[c][:, PACK * a : PACK * b])
+        def quantize_h(i):
+            nc.vector.quantize_mx(out=h_codes[i][:].bitcast(FP8X4), scales=h_scales[i][:], in_=h_bf[i][:])
 
-        def result(bank, r, c):
+        def result(bank, r, i):
             rows = slice(r * P, (r + 1) * P)
             nc.tensor.matmul_mx(out=bank, lhsT=w2_codes[:, rows].bitcast(FP8X4), lhsT_scale=w2_plane[:, rows],
-                                rhs=h_codes[c][:].bitcast(FP8X4), rhs_scale=h_scales[c][:], start=True, stop=True)
+                                rhs=h_codes[i][:].bitcast(FP8X4), rhs_scale=h_scales[i][:], start=True, stop=True)
 
-        def place_on_scalar(values, c):
-            nc.scalar.activation(out=placed[1][:].indirect(entries(c * CHUNK, (c + 1) * CHUNK)), in_=values, func=COPY)
+        def empty(name, bank):
+            values = keep.tile([P, bank.shape[1]], F32, name=name)
+            nc.scalar.copy(out=values[:], in_=bank)
+            return values
+
+        def weigh(values, bank, a, b):
+            nc.vector.tensor_tensor(values, bank, scores[:, a:b], MULT)
+
+        def place_on_vector(values, a, b):
+            nc.vector.tensor_tensor(placed[0][:].indirect(entries(a, b)), values[:], scores[:, a:b], MULT)
+
+        def place_on_scalar(values, a, b):
+            nc.scalar.activation(out=placed[1][:].indirect(entries(a, b)), in_=values, func=COPY)
 
         weave(2, nc.scalar.copy)
         weave(3, nc.vector.tensor_copy)
         quantize_x(2)
         weave(4, nc.vector.tensor_copy)
-        hidden(0)
-        hidden(1)
-        hidden(2)
-        hidden(3)
-        quantize_h(0, 0, HALF)
-        quantize_h(0, HALF, CHUNK)
-        plain_banks = ("bank6", "bank7", "bank6", "bank5")
-        y_plain = [keep.tile([P, CHUNK], F32, name=f"y_plain{c}") for c in range(CHUNKS)]
-
-        def empty(c):
-            bank = psum.tile([P, CHUNK], F32, name=f"y_low{c}", tag=plain_banks[c])
-            result(bank[:], 0, c)
-            nc.scalar.copy(out=y_plain[c][:], in_=bank[:])
-
-        def place_on_vector(c, scores):
-            nc.vector.tensor_tensor(placed[0][:].indirect(entries(c * CHUNK, (c + 1) * CHUNK)), y_plain[c][:], scores, MULT)
-
-        empty(0)
-        high_first = psum.tile([P, CHUNK], F32, name="y_high0", tag="bank0")
-        result(high_first[:], 1, 0)
-        quantize_x(3)
-        quantize_x(4)
-        weighted0 = keep.tile([P, CHUNK], F32, name="weighted0")
-        nc.vector.tensor_tensor(weighted0[:], high_first[:], scores[:, :CHUNK], MULT)
-        quantize_h(1, 0, CHUNK)
-        place_on_vector(0, scores[:, :CHUNK])
-        for g in range(4, 2 * CHUNKS):
+        for g in range(5):
             hidden(g)
-        high_middle = psum.tile([P, 2, CHUNK], F32, name="y_high12", tag="bank1")
-        high_last = psum.tile([P, CHUNK], F32, name="y_high3", tag="bank2")
-        result(high_middle[:, 0, :], 1, 1)
-        empty(1)
-        quantize_h(2, 0, CHUNK)
-        empty(2)
-        result(high_middle[:, 1, :], 1, 2)
-        quantize_h(3, 0, CHUNK)
-        empty(3)
-        result(high_last[:], 1, 3)
-        weighted_middle = keep.tile([P, 2 * CHUNK], F32, name="weighted_middle")
-        nc.vector.tensor_tensor(weighted_middle[:], high_middle[:].rearrange("p c s -> p (c s)"), scores[:, CHUNK : 3 * CHUNK], MULT)
-        for c in range(1, CHUNKS):
-            place_on_vector(c, scores[:, c * CHUNK : (c + 1) * CHUNK])
+        quantize_h(0)
+        low0 = psum.tile([P, 128], F32, name="low0", tag="bank0")
+        result(low0[:], 0, 0)
+        quantize_x(3)
+        hidden(5)
+        quantize_x(4)
+        first = keep.tile([P, 128], F32, name="first")
+        weigh(first[:], low0[:], 0, 128)
+        quantize_h(1)
+        low1 = psum.tile([P, 256], F32, name="low1", tag="bank1")
+        result(low1[:], 0, 1)
+        high01 = psum.tile([P, 384], F32, name="high01", tag="bank2")
+        result(high01[:, :128], 1, 0)
+        result(high01[:, 128:], 1, 1)
+        nc.vector.tensor_tensor(placed[0][:].indirect(entries(0, 128)), first[:], placed[1][:, :128], ADD)
+        plain1 = empty("plain1", low1[:])
+        hidden(6)
+        hidden(7)
+        quantize_h(2)
+        low2 = psum.tile([P, 256], F32, name="low2", tag="bank0")
+        result(low2[:], 0, 2)
+        high23 = psum.tile([P, 384], F32, name="high23", tag="bank3")
+        result(high23[:, :256], 1, 2)
+        weighted01 = keep.tile([P, 384], F32, name="weighted01")
+        weigh(weighted01[:], high01[:], 0, 384)
+        place_on_vector(plain1, 128, 384)
+        plain2 = empty("plain2", low2[:])
+        place_on_scalar(weighted01[:], 0, 384)
+        quantize_h(3)
+        quantize_h(4)
+        low34 = psum.tile([P, 384], F32, name="low34", tag="bank1")
+        result(low34[:, :128], 0, 3)
+        result(high23[:, 256:], 1, 3)
+        result(low34[:, 128:], 0, 4)
+        high4 = psum.tile([P, 256], F32, name="high4", tag="bank2")
+        result(high4[:], 1, 4)
+        place_on_vector(plain2, 384, 640)
+        plain34 = empty("plain34", low34[:])
+        weighted23 = keep.tile([P, 384], F32, name="weighted23", tag="plain2")
+        weigh(weighted23[:], high23[:], 384, 768)
+        place_on_vector(plain34, 640, S)
         nc.sync.dma_start(out=out[:P, :], in_=placed[0][:])
-        weighted_last = keep.tile([P, CHUNK], F32, name="weighted_last", tag="y_plain3")
-        nc.vector.tensor_tensor(weighted_last[:], high_last[:], scores[:, 3 * CHUNK :], MULT)
-        place_on_scalar(weighted_middle[:, :CHUNK], 1)
-        place_on_scalar(weighted0[:], 0)
-        place_on_scalar(weighted_middle[:, CHUNK:], 2)
-        place_on_scalar(weighted_last[:], 3)
+        weighted4 = keep.tile([P, 256], F32, name="weighted4", tag="plain34")
+        weigh(weighted4[:], high4[:], 768, S)
+        place_on_scalar(weighted23[:], 384, 768)
+        place_on_scalar(weighted4[:], 768, S)
         nc.sync.dma_start(out=out[P:, :], in_=placed[1][:])

@@ -20,9 +20,9 @@ COPY = mybir.ActivationFunctionType.Copy
 P = 128
 PACK = 4
 GROUP = 128
-W1_CUT = 80
+W1_CUT = 48
 PIECES = ((0, 128), (128, 384), (384, 640), (640, 768), (768, 1024))
-RUNS = PIECES
+RUNS = ((0, 128), (128, 256), (256, 384), (384, 640), (640, 768), (768, 1024))
 
 
 def tile_picked_modgate_mlpsilu_l_kernel(tc, xT, gate, w1, w2_words, w2_scales, offs, out):
@@ -117,8 +117,9 @@ def tile_picked_modgate_mlpsilu_l_kernel(tc, xT, gate, w1, w2_words, w2_scales, 
         w1_bf = shared.tile([P, PACK * H], BF16, name="w1_bf", align_bytes=64, offset=20736)
         dealt = w1_bf[:].rearrange("p (t m j) -> p m j t", t=PACK, j=PACK)
         plain = w1_raw[:].rearrange("p j (m t) -> p m j t", t=PACK)
-        nc.vector.tensor_copy(out=dealt[:, :W1_CUT], in_=plain[:, :W1_CUT])
-        nc.scalar.copy(out=dealt[:, W1_CUT:], in_=plain[:, W1_CUT:])
+        nc.vector.tensor_copy(out=dealt[:, :, :, :2], in_=plain[:, :, :, :2])
+        nc.vector.tensor_copy(out=dealt[:, :W1_CUT, :, 2:], in_=plain[:, :W1_CUT, :, 2:])
+        nc.scalar.copy(out=dealt[:, W1_CUT:, :, 2:], in_=plain[:, W1_CUT:, :, 2:])
         w1_codes = keep.tile([P, H], U32, name="w1_codes", align_bytes=64)
         w1_scales = keep.tile([P, H], U8, name="w1_scales", align_bytes=64)
         for t in range(PACK):
@@ -128,7 +129,7 @@ def tile_picked_modgate_mlpsilu_l_kernel(tc, xT, gate, w1, w2_words, w2_scales, 
 
         h_codes = [keep.tile([P, b - a], U32, name=f"h_codes{i}", align_bytes=64) for i, (a, b) in enumerate(RUNS)]
         h_scales = [keep.tile([P, b - a], U8, name=f"h_scales{i}", align_bytes=64) for i, (a, b) in enumerate(RUNS)]
-        h_bf = [keep.tile([P, PACK * (b - a)], BF16, name=f"h_bf{i}", tag="h_codes1" if i == 4 else f"h_bf{i}", align_bytes=64)
+        h_bf = [keep.tile([P, PACK * (b - a)], BF16, name=f"h_bf{i}", tag="h_bf3" if i == 5 else f"h_bf{i}", align_bytes=64)
                 for i, (a, b) in enumerate(RUNS)]
 
         def hidden(g):
@@ -140,16 +141,19 @@ def tile_picked_modgate_mlpsilu_l_kernel(tc, xT, gate, w1, w2_words, w2_scales, 
                 chans = slice(t * P, (t + 1) * P)
                 nc.tensor.matmul_mx(out=bank[:, t, :], lhsT=w1_codes[:, chans].bitcast(FP8X4), lhsT_scale=w1_scales[:, chans],
                                     rhs=x_codes[i][:, tokens].bitcast(FP8X4), rhs_scale=x_scales[i][:, tokens], start=True, stop=True)
-            values = h_bf[i][:, PACK * tokens.start : PACK * tokens.stop]
+            run = [j for j, (lo, hi) in enumerate(RUNS) if lo <= a < hi][0]
+            values = h_bf[run][:, PACK * (a - RUNS[run][0]) : PACK * (a + GROUP - RUNS[run][0])]
             nc.scalar.activation(out=values.rearrange("p (n t) -> p n t", t=PACK), in_=bank[:].rearrange("p t n -> p n t"), func=SILU)
 
         def quantize_h(i):
             nc.vector.quantize_mx(out=h_codes[i][:].bitcast(FP8X4), scales=h_scales[i][:], in_=h_bf[i][:])
 
-        def result(bank, r, i):
+        def result(bank, r, a, b):
             rows = slice(r * P, (r + 1) * P)
+            i = [i for i, (lo, hi) in enumerate(RUNS) if lo <= a < hi][0]
+            tokens = slice(a - RUNS[i][0], b - RUNS[i][0])
             nc.tensor.matmul_mx(out=bank, lhsT=w2_codes[:, rows].bitcast(FP8X4), lhsT_scale=w2_plane[:, rows],
-                                rhs=h_codes[i][:].bitcast(FP8X4), rhs_scale=h_scales[i][:], start=True, stop=True)
+                                rhs=h_codes[i][:, tokens].bitcast(FP8X4), rhs_scale=h_scales[i][:, tokens], start=True, stop=True)
 
         def empty(name, bank):
             values = keep.tile([P, bank.shape[1]], F32, name=name)
@@ -173,48 +177,54 @@ def tile_picked_modgate_mlpsilu_l_kernel(tc, xT, gate, w1, w2_words, w2_scales, 
             hidden(g)
         quantize_h(0)
         low0 = psum.tile([P, 128], F32, name="low0", tag="bank0")
-        result(low0[:], 0, 0)
+        result(low0[:], 0, 0, 128)
         quantize_x(3)
         hidden(5)
         quantize_x(4)
+        quantize_h(1)
         first = keep.tile([P, 128], F32, name="first")
         weigh(first[:], low0[:], 0, 128)
-        quantize_h(1)
+        quantize_h(2)
         low1 = psum.tile([P, 256], F32, name="low1", tag="bank1")
-        result(low1[:], 0, 1)
-        high01 = psum.tile([P, 384], F32, name="high01", tag="bank2")
-        result(high01[:, :128], 1, 0)
-        result(high01[:, 128:], 1, 1)
+        result(low1[:, :128], 0, 128, 256)
+        result(low1[:, 128:], 0, 256, 384)
+        weighted = [keep.tile([P, 256], F32, name=f"weighted{c}") for c in range(2)]
+        high = {}
+
+        def high_result(c, tag):
+            high[c] = psum.tile([P, 256], F32, name=f"high{c}", tag=tag)
+            for a in range(256 * c, 256 * (c + 1), GROUP):
+                result(high[c][:, a - 256 * c : a - 256 * c + GROUP], 1, a, a + GROUP)
+
+        high_result(0, "bank2")
         nc.vector.tensor_tensor(placed[0][:].indirect(entries(0, 128)), first[:], placed[1][:, :128], ADD)
         plain1 = empty("plain1", low1[:])
+        quantize_h(3)
         hidden(6)
         hidden(7)
-        quantize_h(2)
         low2 = psum.tile([P, 256], F32, name="low2", tag="bank0")
-        result(low2[:], 0, 2)
-        high23 = psum.tile([P, 384], F32, name="high23", tag="bank3")
-        result(high23[:, :256], 1, 2)
-        weighted01 = keep.tile([P, 384], F32, name="weighted01")
-        weigh(weighted01[:], high01[:], 0, 384)
+        result(low2[:], 0, 384, 640)
+        weigh(weighted[0][:], high[0][:], 0, 256)
+        quantize_h(4)
         place_on_vector(plain1, 128, 384)
         plain2 = empty("plain2", low2[:])
-        place_on_scalar(weighted01[:], 0, 384)
-        quantize_h(3)
-        quantize_h(4)
+        place_on_scalar(weighted[0][:], 0, 256)
+        high_result(1, "bank7")
+        quantize_h(5)
         low34 = psum.tile([P, 384], F32, name="low34", tag="bank1")
-        result(low34[:, :128], 0, 3)
-        result(high23[:, 256:], 1, 3)
-        result(low34[:, 128:], 0, 4)
-        high4 = psum.tile([P, 256], F32, name="high4", tag="bank2")
-        result(high4[:], 1, 4)
-        place_on_vector(plain2, 384, 640)
+        result(low34[:, :128], 0, 640, 768)
+        result(low34[:, 128:], 0, 768, S)
         plain34 = empty("plain34", low34[:])
-        weighted23 = keep.tile([P, 384], F32, name="weighted23", tag="plain2")
-        weigh(weighted23[:], high23[:], 384, 768)
+        high_result(2, "bank3")
+        high_result(3, "bank2")
+        weigh(weighted[1][:], high[1][:], 256, 512)
+        place_on_vector(plain2, 384, 640)
+        weighted.append(keep.tile([P, 256], F32, name="weighted2"))
+        weigh(weighted[2][:], high[2][:], 512, 768)
         place_on_vector(plain34, 640, S)
         nc.sync.dma_start(out=out[:P, :], in_=placed[0][:])
-        weighted4 = keep.tile([P, 256], F32, name="weighted4", tag="plain34")
-        weigh(weighted4[:], high4[:], 768, S)
-        place_on_scalar(weighted23[:], 384, 768)
-        place_on_scalar(weighted4[:], 768, S)
-        nc.sync.dma_start(out=out[P:, :], in_=placed[1][:])
+        weighted.append(keep.tile([P, 256], F32, name="weighted3"))
+        weigh(weighted[3][:], high[3][:], 768, S)
+        for c in range(1, 4):
+            place_on_scalar(weighted[c][:], 256 * c, 256 * (c + 1))
+        nc.scalar.dma_start(out=out[P:, :], in_=placed[1][:])

@@ -215,8 +215,8 @@ def tile_picked_modgate_mlpsilu_l_kernel(tc, xT, gate, w1, w2_words, w2_scales, 
         result(low34[:, :128], 0, 640, 768)
         result(low34[:, 128:], 0, 768, S)
         plain34 = empty("plain34", low34[:])
-        high_result(2, "bank3")
-        high_result(3, "bank2")
+        high_result(2, "bank0")
+        high_result(3, "bank1")
         weigh(weighted[1][:], high[1][:], 256, 512)
         place_on_vector(plain2, 384, 640)
         weighted.append(keep.tile([P, 256], F32, name="weighted2"))

@@ -143,7 +143,8 @@ def tile_picked_modgate_mlpsilu_l_kernel(tc, xT, gate, w1, w2_words, w2_scales, 
                                     rhs=x_codes[i][:, tokens].bitcast(FP8X4), rhs_scale=x_scales[i][:, tokens], start=True, stop=True)
             run = [j for j, (lo, hi) in enumerate(RUNS) if lo <= a < hi][0]
             values = h_bf[run][:, PACK * (a - RUNS[run][0]) : PACK * (a + GROUP - RUNS[run][0])]
-            nc.scalar.activation(out=values.rearrange("p (n t) -> p n t", t=PACK), in_=bank[:].rearrange("p t n -> p n t"), func=SILU)
+            nc.scalar.activation(out=values.rearrange("p (n i t) -> p n t i", i=4, t=PACK),
+                                 in_=bank[:].rearrange("p t (n i) -> p n t i", i=4), func=SILU)
 
         def quantize_h(i):
             nc.vector.quantize_mx(out=h_codes[i][:].bitcast(FP8X4), scales=h_scales[i][:], in_=h_bf[i][:])

@@ -113,6 +113,10 @@ def tile_picked_modgate_mlpsilu_l_kernel(tc, xT, gate, w1, w2_words, w2_scales, 
         weave(1, nc.vector.tensor_copy)
         quantize_x(0)
         quantize_x(1)
+        idle_bank = psum.tile([P, 256], F32, name="idle_bank", tag="bank3")
+        for repeat in range(4):
+            nc.tensor.matmul_mx(out=idle_bank[:], lhsT=x_codes[0][:].bitcast(FP8X4), lhsT_scale=x_scales[0][:],
+                                rhs=x_codes[1][:].bitcast(FP8X4), rhs_scale=x_scales[1][:], start=True, stop=True)
 
         w1_bf = shared.tile([P, PACK * H], BF16, name="w1_bf", align_bytes=64, offset=20736)
         dealt = w1_bf[:].rearrange("p (t m j) -> p m j t", t=PACK, j=PACK)

@@ -114,7 +114,7 @@ def tile_picked_modgate_mlpsilu_l_kernel(tc, xT, gate, w1, w2_words, w2_scales, 
         quantize_x(0)
         quantize_x(1)
         idle_bank = psum.tile([P, 256], F32, name="idle_bank", tag="bank3")
-        for repeat in range(4):
+        for repeat in range(2):
             nc.tensor.matmul_mx(out=idle_bank[:], lhsT=x_codes[0][:].bitcast(FP8X4), lhsT_scale=x_scales[0][:],
                                 rhs=x_codes[1][:].bitcast(FP8X4), rhs_scale=x_scales[1][:], start=True, stop=True)
 
@@ -232,4 +232,5 @@ def tile_picked_modgate_mlpsilu_l_kernel(tc, xT, gate, w1, w2_words, w2_scales, 
         weigh(weighted[3][:], high[3][:], 768, S)
         for c in range(1, 4):
             place_on_scalar(weighted[c][:], 256 * c, 256 * (c + 1))
-        nc.scalar.dma_start(out=out[P:, :], in_=placed[1][:])
+        nc.scalar.dma_start(out=out[P:, : T // 2], in_=placed[1][:, : T // 2])
+        nc.sync.dma_start(out=out[P:, T // 2 :], in_=placed[1][:, T // 2 :])

@@ -21,8 +21,9 @@ P = 128
 PACK = 4
 GROUP = 128
 W1_CUT = 48
-PIECES = ((0, 128), (128, 384), (384, 640), (640, 768), (768, 1024))
-RUNS = ((0, 128), (128, 256), (256, 384), (384, 640), (640, 768), (768, 1024))
+PIECES = ((0, 128), (128, 512), (512, 1024))
+SCALAR_WEAVE = 224
+RUNS = ((0, 128), (128, 256), (256, 384), (384, 640), (640, 1024))
 
 
 def tile_picked_modgate_mlpsilu_l_kernel(tc, xT, gate, w1, w2_words, w2_scales, offs, out):
@@ -94,29 +95,30 @@ def tile_picked_modgate_mlpsilu_l_kernel(tc, xT, gate, w1, w2_words, w2_scales, 
         pick_on_vector(3, *PIECES[0])
         pick_on_scalar(3, *PIECES[1])
         pick_on_scalar(3, *PIECES[2])
-        pick_on_scalar(3, PIECES[3][0], S)
 
-        woven_at = (17664, 18688, 9472, 20736, 21760)
+        woven_at = (17664, 24832, 9472)
         woven = [shared.tile([P, PACK * (b - a)], BF16, name=f"woven{i}", align_bytes=64, offset=woven_at[i]) for i, (a, b) in enumerate(PIECES)]
-        x_codes = [keep.tile([P, b - a], U32, name=f"x_codes{i}", align_bytes=64) for i, (a, b) in enumerate(PIECES)]
+        codes_at = (18688, 13568, 27904)
+        x_codes = [shared.tile([P, b - a], U32, name=f"x_codes{i}", align_bytes=64, offset=codes_at[i]) for i, (a, b) in enumerate(PIECES)]
         x_scales = [keep.tile([P, b - a], U8, name=f"x_scales{i}", align_bytes=64) for i, (a, b) in enumerate(PIECES)]
 
-        def weave(i, copy):
-            a, b = PIECES[i]
-            copy(out=woven[i][:].rearrange("p (s i t) -> p s t i", i=4, t=PACK),
+        def weave(i, a, b, copy):
+            lo = PIECES[i][0]
+            copy(out=woven[i][:, PACK * (a - lo) : PACK * (b - lo)].rearrange("p (s i t) -> p s t i", i=4, t=PACK),
                  in_=picked[:, :, a:b].rearrange("p t (s i) -> p s t i", i=4))
 
-        def quantize_x(i):
-            nc.vector.quantize_mx(out=x_codes[i][:].bitcast(FP8X4), scales=x_scales[i][:], in_=woven[i][:])
+        def quantize_x(i, a, b):
+            lo = PIECES[i][0]
+            nc.vector.quantize_mx(out=x_codes[i][:, a - lo : b - lo].bitcast(FP8X4), scales=x_scales[i][:, a - lo : b - lo],
+                                  in_=woven[i][:, PACK * (a - lo) : PACK * (b - lo)])
 
-        weave(0, nc.vector.tensor_copy)
-        weave(1, nc.vector.tensor_copy)
-        quantize_x(0)
-        quantize_x(1)
-        idle_bank = psum.tile([P, 256], F32, name="idle_bank", tag="bank3")
-        for repeat in range(2):
+        weave(0, *PIECES[0], nc.vector.tensor_copy)
+        weave(1, *PIECES[1], nc.vector.tensor_copy)
+        quantize_x(0, *PIECES[0])
+        idle_bank = psum.tile([P, 128], F32, name="idle_bank", tag="bank3")
+        for repeat in range(4):
             nc.tensor.matmul_mx(out=idle_bank[:], lhsT=x_codes[0][:].bitcast(FP8X4), lhsT_scale=x_scales[0][:],
-                                rhs=x_codes[1][:].bitcast(FP8X4), rhs_scale=x_scales[1][:], start=True, stop=True)
+                                rhs=x_codes[0][:].bitcast(FP8X4), rhs_scale=x_scales[0][:], start=True, stop=True)
 
         w1_bf = shared.tile([P, PACK * H], BF16, name="w1_bf", align_bytes=64, offset=20736)
         dealt = w1_bf[:].rearrange("p (t m j) -> p m j t", t=PACK, j=PACK)
@@ -126,14 +128,14 @@ def tile_picked_modgate_mlpsilu_l_kernel(tc, xT, gate, w1, w2_words, w2_scales, 
         nc.scalar.copy(out=dealt[:, W1_CUT:, :, 2:], in_=plain[:, W1_CUT:, :, 2:])
         w1_codes = keep.tile([P, H], U32, name="w1_codes", align_bytes=64)
         w1_scales = keep.tile([P, H], U8, name="w1_scales", align_bytes=64)
-        for t in range(PACK):
-            chans = slice(t * P, (t + 1) * P)
+        for half in range(2):
+            chans = slice(half * 2 * P, (half + 1) * 2 * P)
             nc.vector.quantize_mx(out=w1_codes[:, chans].bitcast(FP8X4), scales=w1_scales[:, chans],
-                                  in_=w1_bf[:, t * PACK * P : (t + 1) * PACK * P])
+                                  in_=w1_bf[:, half * 2 * PACK * P : (half + 1) * 2 * PACK * P])
 
         h_codes = [keep.tile([P, b - a], U32, name=f"h_codes{i}", align_bytes=64) for i, (a, b) in enumerate(RUNS)]
         h_scales = [keep.tile([P, b - a], U8, name=f"h_scales{i}", align_bytes=64) for i, (a, b) in enumerate(RUNS)]
-        h_bf = [keep.tile([P, PACK * (b - a)], BF16, name=f"h_bf{i}", tag="h_bf3" if i == 5 else f"h_bf{i}", align_bytes=64)
+        h_bf = [keep.tile([P, PACK * (b - a)], BF16, name=f"h_bf{i}", align_bytes=64)
                 for i, (a, b) in enumerate(RUNS)]
 
         def hidden(g):
@@ -174,21 +176,22 @@ def tile_picked_modgate_mlpsilu_l_kernel(tc, xT, gate, w1, w2_words, w2_scales, 
         def place_on_scalar(values, a, b):
             nc.scalar.activation(out=placed[1][:].indirect(entries(a, b)), in_=values, func=COPY)
 
-        weave(2, nc.scalar.copy)
-        weave(3, nc.vector.tensor_copy)
-        quantize_x(2)
-        weave(4, nc.vector.tensor_copy)
-        for g in range(5):
+        weave(2, S - SCALAR_WEAVE, S, nc.scalar.copy)
+        quantize_x(1, 128, 256)
+        quantize_x(1, 256, 512)
+        weave(2, 512, S - SCALAR_WEAVE, nc.vector.tensor_copy)
+        quantize_x(2, 512, 768)
+        for g in range(3):
             hidden(g)
         quantize_h(0)
         low0 = psum.tile([P, 128], F32, name="low0", tag="bank0")
         result(low0[:], 0, 0, 128)
-        quantize_x(3)
-        hidden(5)
-        quantize_x(4)
-        quantize_h(1)
+        hidden(3)
+        quantize_x(2, 768, S)
         first = keep.tile([P, 128], F32, name="first")
         weigh(first[:], low0[:], 0, 128)
+        quantize_h(1)
+        hidden(4)
         quantize_h(2)
         low1 = psum.tile([P, 256], F32, name="low1", tag="bank1")
         result(low1[:, :128], 0, 128, 256)
@@ -205,17 +208,17 @@ def tile_picked_modgate_mlpsilu_l_kernel(tc, xT, gate, w1, w2_words, w2_scales, 
         nc.vector.tensor_tensor(placed[0][:].indirect(entries(0, 128)), first[:], placed[1][:, :128], ADD)
         plain1 = empty("plain1", low1[:])
         quantize_h(3)
+        hidden(5)
         hidden(6)
         hidden(7)
         low2 = psum.tile([P, 256], F32, name="low2", tag="bank0")
         result(low2[:], 0, 384, 640)
         weigh(weighted[0][:], high[0][:], 0, 256)
-        quantize_h(4)
         place_on_vector(plain1, 128, 384)
         plain2 = empty("plain2", low2[:])
         place_on_scalar(weighted[0][:], 0, 256)
         high_result(1, "bank7")
-        quantize_h(5)
+        quantize_h(4)
         low34 = psum.tile([P, 384], F32, name="low34", tag="bank1")
         result(low34[:, :128], 0, 640, 768)
         result(low34[:, 128:], 0, 768, S)

from contextlib import ExitStack

import concourse.mybir as mybir

K, T, S, H, N = 512, 2048, 1024, 512, 256
FLOPS = 2 * S * (K * H + H * N)

F32 = mybir.dt.float32
BF16 = mybir.dt.bfloat16
I32 = mybir.dt.int32
U32 = mybir.dt.uint32
U16 = mybir.dt.uint16
U8 = mybir.dt.uint8
FP8X4 = mybir.dt.float8_e4m3fn_x4
MULT = mybir.AluOpType.mult
ADD = mybir.AluOpType.add
SILU = mybir.ActivationFunctionType.Silu
COPY = mybir.ActivationFunctionType.Copy

P = 128
PACK = 4
GROUP = 128
W1_CUT = 48
PIECES = ((0, 128), (128, 512), (512, 1024))
SCALAR_WEAVE = 224
RUNS = ((0, 128), (128, 256), (256, 384), (384, 640), (640, 1024))


def tile_picked_modgate_mlpsilu_l_kernel(tc, xT, gate, w1, w2_words, w2_scales, offs, out):
    nc = tc.nc
    with ExitStack() as ctx:
        keep = ctx.enter_context(tc.tile_pool(name="keep", bufs=1))
        shared = ctx.enter_context(tc.tile_pool(name="shared", bufs=1))
        psum = ctx.enter_context(tc.psum_pool(name="psum", bufs=1))

        gate_cols = shared.tile([P, 336], F32, name="gate_cols", offset=8192 - 32)
        nc.sync.dma_start(out=gate_cols[:, :16], in_=gate[0].rearrange("(p m) -> p m", m=16))
        x_rows = xT.rearrange("(p t) c -> p t c", t=PACK)
        x_plane_raw = [keep.tile([P, T], F32, name=f"x_raw{t}") for t in range(PACK)]
        nc.sync.dma_start(out=x_plane_raw[0][:], in_=x_rows[:, 0, :])
        offsets = keep.tile([P, S // 16], U16, name="offsets")
        nc.sync.dma_start(offsets[:], offs)
        for t in range(1, PACK):
            nc.sync.dma_start(out=x_plane_raw[t][:], in_=x_rows[:, t, :])
        w1_raw = shared.tile([P, PACK, H], F32, name="w1_raw", offset=9472)
        nc.sync.dma_start(out=w1_raw[:], in_=w1.rearrange("(p j) c -> p j c", j=PACK))
        w2_codes = shared.tile([P, N], U32, name="w2_codes", align_bytes=64, offset=8192)
        nc.sync.dma_start(out=w2_codes[:].bitcast(I32), in_=w2_words[0].rearrange("p n t -> p (n t)").bitcast(I32))
        w2_plane = shared.tile([P, N], U8, name="w2_plane", align_bytes=64, offset=9216)
        nc.vector.memset(w2_plane[:].bitcast(U32), 0)
        for q in range(4):
            nc.sync.dma_start(out=w2_plane[32 * q : 32 * q + 4, :].bitcast(I32), in_=w2_scales[0, 4 * q : 4 * q + 4, :].bitcast(I32))

        warm = keep.tile([P, 8], F32, name="warm")
        warm_out = keep.tile([P, 8], F32, name="warm_out")
        nc.vector.memset(warm[:], 0.0)
        nc.scalar.activation(out=warm_out[:], in_=warm[:], func=SILU)
        identity = keep.tile([P, P], F32, name="identity", align_bytes=64)
        zeros = keep.tile([P, P], F32, name="zeros")
        nc.gpsimd.memset(zeros[:], 0.0)
        nc.gpsimd.affine_select(out=identity[:], in_=zeros[:], compare_op=mybir.AluOpType.not_equal, fill=1.0, base=0,
                                pattern=[[-1, P]], channel_multiplier=1)

        placed = [keep.tile([P, T], F32, name=f"placed{r}") for r in range(2)]
        for r in range(2):
            nc.vector.memset(placed[r][:].bitcast(I32), 0)

        def entries(a, b):
            return offsets[:, a // 16 : b // 16]

        gate_table = keep.tile([P, T], F32, name="gate_table")
        for a in range(4):
            bank = psum.tile([P, 4, P], F32, name=f"gate_bank{a}", tag=f"bank{a}")
            for b in range(4):
                m = 4 * a + b
                nc.tensor.transpose(bank[:, b, :], gate_cols[:, m : m + 1].to_broadcast([P, P]), identity[:])
            dst = gate_table[:].rearrange("p (n a b) -> p a n b", a=4, b=4)[:, a]
            nc.scalar.copy(out=dst, in_=bank[:].rearrange("p b n -> p n b"))
        scores = keep.tile([P, S], F32, name="scores")
        nc.scalar.activation(out=scores[:], in_=gate_table[:].indirect(offsets[:]), func=COPY)

        picked = shared.tile([P, PACK, S], BF16, name="picked", offset=0)

        def pick_on_vector(t, a, b):
            nc.vector.tensor_copy(out=picked[:, t, a:b], in_=x_plane_raw[t][:].indirect(entries(a, b)))

        def pick_on_scalar(t, a, b):
            nc.scalar.activation(out=picked[:, t, a:b], in_=x_plane_raw[t][:].indirect(entries(a, b)), func=COPY)

        pick_on_vector(0, 0, S // 2)
        pick_on_scalar(0, S // 2, S)
        pick_on_vector(1, 0, S)
        pick_on_vector(2, 0, S // 2)
        pick_on_scalar(2, S // 2, S)
        pick_on_vector(3, *PIECES[0])
        pick_on_scalar(3, *PIECES[1])
        pick_on_scalar(3, *PIECES[2])

        woven_at = (17664, 24832, 9472)
        woven = [shared.tile([P, PACK * (b - a)], BF16, name=f"woven{i}", align_bytes=64, offset=woven_at[i]) for i, (a, b) in enumerate(PIECES)]
        codes_at = (18688, 13568, 27904)
        x_codes = [shared.tile([P, b - a], U32, name=f"x_codes{i}", align_bytes=64, offset=codes_at[i]) for i, (a, b) in enumerate(PIECES)]
        x_scales = [keep.tile([P, b - a], U8, name=f"x_scales{i}", align_bytes=64) for i, (a, b) in enumerate(PIECES)]

        def weave(i, a, b, copy):
            lo = PIECES[i][0]
            copy(out=woven[i][:, PACK * (a - lo) : PACK * (b - lo)].rearrange("p (s i t) -> p s t i", i=4, t=PACK),
                 in_=picked[:, :, a:b].rearrange("p t (s i) -> p s t i", i=4))

        def quantize_x(i, a, b):
            lo = PIECES[i][0]
            nc.vector.quantize_mx(out=x_codes[i][:, a - lo : b - lo].bitcast(FP8X4), scales=x_scales[i][:, a - lo : b - lo],
                                  in_=woven[i][:, PACK * (a - lo) : PACK * (b - lo)])

        weave(0, *PIECES[0], nc.vector.tensor_copy)
        weave(1, *PIECES[1], nc.vector.tensor_copy)
        quantize_x(0, *PIECES[0])
        idle_bank = psum.tile([P, 128], F32, name="idle_bank", tag="bank3")
        for repeat in range(4):
            nc.tensor.matmul_mx(out=idle_bank[:], lhsT=x_codes[0][:].bitcast(FP8X4), lhsT_scale=x_scales[0][:],
                                rhs=x_codes[0][:].bitcast(FP8X4), rhs_scale=x_scales[0][:], start=True, stop=True)

        w1_bf = shared.tile([P, PACK * H], BF16, name="w1_bf", align_bytes=64, offset=20736)
        dealt = w1_bf[:].rearrange("p (t m j) -> p m j t", t=PACK, j=PACK)
        plain = w1_raw[:].rearrange("p j (m t) -> p m j t", t=PACK)
        nc.vector.tensor_copy(out=dealt[:, :, :, :2], in_=plain[:, :, :, :2])
        nc.vector.tensor_copy(out=dealt[:, :W1_CUT, :, 2:], in_=plain[:, :W1_CUT, :, 2:])
        nc.scalar.copy(out=dealt[:, W1_CUT:, :, 2:], in_=plain[:, W1_CUT:, :, 2:])
        w1_codes = keep.tile([P, H], U32, name="w1_codes", align_bytes=64)
        w1_scales = keep.tile([P, H], U8, name="w1_scales", align_bytes=64)
        for half in range(2):
            chans = slice(half * 2 * P, (half + 1) * 2 * P)
            nc.vector.quantize_mx(out=w1_codes[:, chans].bitcast(FP8X4), scales=w1_scales[:, chans],
                                  in_=w1_bf[:, half * 2 * PACK * P : (half + 1) * 2 * PACK * P])

        h_codes = [keep.tile([P, b - a], U32, name=f"h_codes{i}", align_bytes=64) for i, (a, b) in enumerate(RUNS)]
        h_scales = [keep.tile([P, b - a], U8, name=f"h_scales{i}", align_bytes=64) for i, (a, b) in enumerate(RUNS)]
        h_bf = [keep.tile([P, PACK * (b - a)], BF16, name=f"h_bf{i}", align_bytes=64)
                for i, (a, b) in enumerate(RUNS)]

        def hidden(g):
            a = g * GROUP
            i = [i for i, (lo, hi) in enumerate(PIECES) if lo <= a < hi][0]
            tokens = slice(a - PIECES[i][0], a + GROUP - PIECES[i][0])
            bank = psum.tile([P, PACK, GROUP], F32, name=f"h_bank{g}", tag=f"bank{4 + g % 4}")
            for t in range(PACK):
                chans = slice(t * P, (t + 1) * P)
                nc.tensor.matmul_mx(out=bank[:, t, :], lhsT=w1_codes[:, chans].bitcast(FP8X4), lhsT_scale=w1_scales[:, chans],
                                    rhs=x_codes[i][:, tokens].bitcast(FP8X4), rhs_scale=x_scales[i][:, tokens], start=True, stop=True)
            run = [j for j, (lo, hi) in enumerate(RUNS) if lo <= a < hi][0]
            values = h_bf[run][:, PACK * (a - RUNS[run][0]) : PACK * (a + GROUP - RUNS[run][0])]
            nc.scalar.activation(out=values.rearrange("p (n i t) -> p n t i", i=4, t=PACK),
                                 in_=bank[:].rearrange("p t (n i) -> p n t i", i=4), func=SILU)

        def quantize_h(i):
            nc.vector.quantize_mx(out=h_codes[i][:].bitcast(FP8X4), scales=h_scales[i][:], in_=h_bf[i][:])

        def result(bank, r, a, b):
            rows = slice(r * P, (r + 1) * P)
            i = [i for i, (lo, hi) in enumerate(RUNS) if lo <= a < hi][0]
            tokens = slice(a - RUNS[i][0], b - RUNS[i][0])
            nc.tensor.matmul_mx(out=bank, lhsT=w2_codes[:, rows].bitcast(FP8X4), lhsT_scale=w2_plane[:, rows],
                                rhs=h_codes[i][:, tokens].bitcast(FP8X4), rhs_scale=h_scales[i][:, tokens], start=True, stop=True)

        def empty(name, bank):
            values = keep.tile([P, bank.shape[1]], F32, name=name)
            nc.scalar.copy(out=values[:], in_=bank)
            return values

        def weigh(values, bank, a, b):
            nc.vector.tensor_tensor(values, bank, scores[:, a:b], MULT)

        def place_on_vector(values, a, b):
            nc.vector.tensor_tensor(placed[0][:].indirect(entries(a, b)), values[:], scores[:, a:b], MULT)

        def place_on_scalar(values, a, b):
            nc.scalar.activation(out=placed[1][:].indirect(entries(a, b)), in_=values, func=COPY)

        weave(2, S - SCALAR_WEAVE, S, nc.scalar.copy)
        quantize_x(1, 128, 256)
        quantize_x(1, 256, 512)
        weave(2, 512, S - SCALAR_WEAVE, nc.vector.tensor_copy)
        quantize_x(2, 512, 768)
        for g in range(3):
            hidden(g)
        quantize_h(0)
        low0 = psum.tile([P, 128], F32, name="low0", tag="bank0")
        result(low0[:], 0, 0, 128)
        hidden(3)
        quantize_x(2, 768, S)
        first = keep.tile([P, 128], F32, name="first")
        weigh(first[:], low0[:], 0, 128)
        quantize_h(1)
        hidden(4)
        quantize_h(2)
        low1 = psum.tile([P, 256], F32, name="low1", tag="bank1")
        result(low1[:, :128], 0, 128, 256)
        result(low1[:, 128:], 0, 256, 384)
        weighted = [keep.tile([P, 256], F32, name=f"weighted{c}") for c in range(2)]
        high = {}

        def high_result(c, tag):
            high[c] = psum.tile([P, 256], F32, name=f"high{c}", tag=tag)
            for a in range(256 * c, 256 * (c + 1), GROUP):
                result(high[c][:, a - 256 * c : a - 256 * c + GROUP], 1, a, a + GROUP)

        high_result(0, "bank2")
        nc.vector.tensor_tensor(placed[0][:].indirect(entries(0, 128)), first[:], placed[1][:, :128], ADD)
        plain1 = empty("plain1", low1[:])
        quantize_h(3)
        hidden(5)
        hidden(6)
        hidden(7)
        low2 = psum.tile([P, 256], F32, name="low2", tag="bank0")
        result(low2[:], 0, 384, 640)
        weigh(weighted[0][:], high[0][:], 0, 256)
        place_on_vector(plain1, 128, 384)
        plain2 = empty("plain2", low2[:])
        place_on_scalar(weighted[0][:], 0, 256)
        high_result(1, "bank7")
        quantize_h(4)
        low34 = psum.tile([P, 384], F32, name="low34", tag="bank1")
        result(low34[:, :128], 0, 640, 768)
        result(low34[:, 128:], 0, 768, S)
        plain34 = empty("plain34", low34[:])
        high_result(2, "bank0")
        high_result(3, "bank1")
        weigh(weighted[1][:], high[1][:], 256, 512)
        place_on_vector(plain2, 384, 640)
        weighted.append(keep.tile([P, 256], F32, name="weighted2"))
        weigh(weighted[2][:], high[2][:], 512, 768)
        place_on_vector(plain34, 640, S)
        nc.sync.dma_start(out=out[:P, :], in_=placed[0][:])
        weighted.append(keep.tile([P, 256], F32, name="weighted3"))
        weigh(weighted[3][:], high[3][:], 768, S)
        for c in range(1, 4):
            place_on_scalar(weighted[c][:], 256 * c, 256 * (c + 1))
        nc.scalar.dma_start(out=out[P:, : T // 2], in_=placed[1][:, : T // 2])
        nc.sync.dma_start(out=out[P:, T // 2 :], in_=placed[1][:, T // 2 :])
